import numpy as np
import ml_dtypes


def mxq(x, axis, fmt="e4m3"):
    dtype, down = {"e4m3": (ml_dtypes.float8_e4m3fn, 7), "e5m2": (ml_dtypes.float8_e5m2, 14)}[fmt]
    v = np.moveaxis(np.asarray(x, np.float32).astype(ml_dtypes.bfloat16).astype(np.float64), axis, -1)
    blocks = v.reshape(v.shape[:-1] + (-1, 32))
    amax = np.abs(blocks).max(-1, keepdims=True)
    byte = np.maximum(np.where(amax > 0, np.frexp(amax)[1] - 1 + 127, 0) - down, 1)
    scale = np.exp2(byte - 127.0)
    codes = (blocks / scale).astype(np.float32).astype(dtype).astype(np.float64)
    return np.moveaxis((codes * scale).reshape(v.shape), -1, axis)


WIDE = False


def mx_kscale(k):
    if not WIDE:
        return np.ones(k)
    levels = np.array([10, -10, 5, -5, 0])
    if k % 512:
        return np.exp2(np.random.permutation(np.resize(levels, k // 32))).repeat(32)
    a = np.empty((k // 512, 16))
    for p in range(k // 512):
        a[p, :8] = np.random.permutation(np.resize(levels, 8))
        for g in range(8):
            far = levels[np.abs(levels - a[p, g]) >= 10]
            a[p, g + 8] = far[np.random.randint(len(far))]
    return np.exp2(a.ravel()).repeat(32)


def f64(x):
    return np.asarray(x).astype(np.float64)


def striped(idx):
    return np.tile(idx.reshape(-1, 16).T, (8, 1)).astype(np.uint16)


def unstriped(offs):
    return offs[:16].T.reshape(-1).astype(np.int64)


E2M1 = np.array([0.0, 0.5, 1.0, 1.5, 2.0, 3.0, 4.0, 6.0, -0.0, -0.5, -1.0, -1.5, -2.0, -3.0, -4.0, -6.0])


def pack_weight(w, fmt):
    k, n = w.shape
    w = f64(np.asarray(w, np.float32).astype(ml_dtypes.bfloat16)).reshape(k // 32, 32, n)
    amax = np.abs(w).max(1)
    if fmt == "e4m3":
        byte = np.frexp(amax)[1] - 1 + 127 - 7
    else:
        mant, ex = np.frexp(amax / 6.0)
        byte = np.where(mant > 0.5, ex, ex - 1) + 127
    byte = np.clip(np.where(amax > 0, byte, 1), 1, 254)
    scaled = (w * np.exp2(127.0 - byte)[:, None, :]).reshape(k, n).astype(np.float32)
    by_word = np.ascontiguousarray(scaled.reshape(k // 512, 128, 4, n).transpose(0, 1, 3, 2))
    if fmt == "e4m3":
        words = by_word.astype(ml_dtypes.float8_e4m3fn).view(np.uint8)
    else:
        c = by_word.astype(ml_dtypes.float4_e2m1fn).view(np.uint8) & 0xF
        words = (c[..., 0::2] | (c[..., 1::2] << 4)).reshape(k // 512, 128, 2 * n)
    return np.ascontiguousarray(words), np.ascontiguousarray(byte.astype(np.uint8).reshape(k // 512, 16, n))


def unpack_weight(words, scales, fmt):
    g, _, n = scales.shape
    words = np.ascontiguousarray(words).reshape(g, 128, n, -1)
    if fmt == "e4m3":
        vals = words.view(ml_dtypes.float8_e4m3fn).astype(np.float64)
    else:
        nib = np.empty((g, 128, n, 4), np.uint8)
        nib[..., 0::2] = words & 0xF
        nib[..., 1::2] = words >> 4
        vals = E2M1[nib]
    vals = vals * np.repeat(np.exp2(scales.astype(np.float64) - 127.0), 8, axis=1)[..., None]
    return vals.transpose(0, 1, 3, 2).reshape(g * 512, n)


K, M, T, S = 1024, 1024, 4096, 1536


def setup_inputs():
    n = np.random.standard_normal
    s = mx_kscale(K)[:, None]
    u = mx_kscale(512)[:, None]
    v = pack_weight(n((K, T)) * s, "e4m3")
    p_w4 = pack_weight(n((K, M)) / np.sqrt(K) / s, "e2m1")
    return {
        "tab_words": v[0],
        "tab_scales": v[1],
        "w4_words": p_w4[0],
        "w4_scales": p_w4[1],
        "down": (n((K, 512)) / np.sqrt(K) / s * u.T).astype(np.float32),
        "up": (0.5 * n((512, M)) / np.sqrt(512) / u).astype(np.float32),
        "rT": n((M, T)).astype(np.float32),
        "offs": striped(np.random.permutation(T)[:S]),
    }


def reference(tab_words, tab_scales, w4_words, w4_scales, down, up, rT, offs):
    tab_ = unpack_weight(tab_words, tab_scales, "e4m3")[:, unstriped(offs)]
    w4_ = unpack_weight(w4_words, w4_scales, "e2m1")
    down_ = mxq(f64(down), 0, "e4m3")
    up_ = mxq(f64(up), 0, "e4m3")
    h_ = mxq(down_.T @ tab_, 0, "e4m3")
    y = w4_.T @ tab_ + up_.T @ h_
    return (y) + f64(rT)[:, unstriped(offs)]

@@ -1,0 +1,193 @@
+from contextlib import ExitStack
+
+import concourse.mybir as mybir
+
+K, M, T, S, R = 1024, 1024, 4096, 1536, 512
+FLOPS = 2 * S * (K * R + K * M + R * M)
+
+F32 = mybir.dt.float32
+BF16 = mybir.dt.bfloat16
+I32 = mybir.dt.int32
+U32 = mybir.dt.uint32
+U16 = mybir.dt.uint16
+U8 = mybir.dt.uint8
+FP8X4 = mybir.dt.float8_e4m3fn_x4
+FP4X4 = mybir.dt.float4_e2m1fn_x4
+ADD = mybir.AluOpType.add
+
+P = 128
+PACK = 4
+K_PASS = P * PACK
+PASSES = K // K_PASS
+BANK = 512
+SLICES = S // BANK
+BLOCKS = M // P
+GROUP = 16
+STREAM_BUFS = 7
+STAGE_BUFS = 4
+
+
+def tile_list_tabres_none_kernel(
+    tc, tab_words, tab_scales, w4_words, w4_scales, down, up, rT, offs, out
+):
+    nc = tc.nc
+    with ExitStack() as ctx:
+        keep = ctx.enter_context(tc.tile_pool(name="keep", bufs=1))
+        stream = ctx.enter_context(tc.tile_pool(name="stream", bufs=STREAM_BUFS))
+        stage = ctx.enter_context(tc.tile_pool(name="stage", bufs=STAGE_BUFS))
+        picked = ctx.enter_context(tc.tile_pool(name="picked", bufs=2))
+        psum_h = ctx.enter_context(tc.psum_pool(name="psum_h", bufs=3))
+        psum_y = ctx.enter_context(tc.psum_pool(name="psum_y", bufs=5))
+
+        offsets = keep.tile([P, S // GROUP], U16, name="offsets")
+        nc.sync.dma_start(offsets[:], offs)
+
+        def listed(lo, hi):
+            return offsets[:, lo // GROUP : hi // GROUP]
+
+        tab_planes = keep.tile([P, PASSES, T // 4], I32, name="tab_planes", align_bytes=64)
+        w4_planes = keep.tile([P, PASSES, M // 4], I32, name="w4_planes", align_bytes=64)
+        nc.vector.memset(tab_planes[:], 0)
+        nc.vector.memset(w4_planes[:], 0)
+
+        def load_planes(engine, planes, scales):
+            rows = scales.bitcast(I32).rearrange("a (q r) c -> r q a c", r=4)
+            for r in range(4):
+                engine.dma_start(out=planes[r:P:32, :, :], in_=rows[r])
+
+        load_planes(nc.scalar, tab_planes, tab_scales)
+        load_planes(nc.scalar, w4_planes, w4_scales)
+
+        def load_table(a):
+            words = stream.tile([P, T], I32, name=f"tab{a}", tag="stream", align_bytes=64)
+            nc.sync.dma_start(out=words[:], in_=tab_words[a].rearrange("p t i -> p (t i)").bitcast(I32))
+            return words
+
+        down_raw = stream.tile([P, PASSES, PACK, R], F32, name="down_raw", tag="stream", align_bytes=64)
+        for a in range(PASSES):
+            nc.sync.dma_start(
+                out=down_raw[:, a, :, :],
+                in_=down[a * K_PASS : (a + 1) * K_PASS, :].rearrange("(p i) r -> p i r", i=PACK),
+            )
+        tab0 = load_table(0)
+        tab1 = load_table(1)
+        up_raw = stream.tile([P, PACK, M], F32, name="up_raw", tag="stream", align_bytes=64)
+        nc.sync.dma_start(out=up_raw[:], in_=up.rearrange("(p i) n -> p i n", i=PACK))
+        w4 = keep.tile([P, PASSES, 2 * M // 4], I32, name="w4", align_bytes=64)
+        nc.sync.dma_start(out=w4[:], in_=w4_words.bitcast(I32).rearrange("a p c -> p a c"))
+        residual = []
+        for b in range(BLOCKS):
+            rows = stream.tile([P, T], F32, name=f"residual{b}", tag="stream", align_bytes=64)
+            nc.sync.dma_start(out=rows[:], in_=rT[b * P : (b + 1) * P, :])
+            residual.append(rows)
+
+        v_words = [keep.tile([P, S], U32, name=f"v_words{a}", align_bytes=64) for a in range(PASSES)]
+        v_scales = [keep.tile([P, S], U8, name=f"v_scales{a}", align_bytes=64) for a in range(PASSES)]
+        for a in range(PASSES):
+            nc.vector.tensor_copy(v_scales[a][:], tab_planes[:, a, :].bitcast(U8).indirect(offsets[:]))
+        nc.vector.tensor_copy(v_words[0][:], tab0[:].bitcast(U32).indirect(offsets[:]))
+
+        down_codes = keep.tile([P, PASSES, R], U32, name="down_codes", align_bytes=64)
+        down_scales = keep.tile([P, PASSES, R], U8, name="down_scales", align_bytes=64)
+        for a in range(PASSES):
+            grouped = stage.tile([P, PACK * R], BF16, name=f"down_bf{a}", tag="stage", align_bytes=64)
+            nc.scalar.copy(
+                out=grouped[:].rearrange("p (t m i) -> p m t i", t=PACK, i=PACK),
+                in_=down_raw[:, a, :, :].rearrange("p i (m t) -> p m t i", t=PACK),
+            )
+            nc.vector.quantize_mx(
+                out=down_codes[:, a, :].bitcast(FP8X4), scales=down_scales[:, a, :], in_=grouped[:]
+            )
+
+        for s in range(SLICES):
+            lo, hi = s * BANK, (s + 1) * BANK
+            nc.vector.tensor_copy(v_words[1][:, lo:hi], tab1[:].bitcast(U32).indirect(listed(lo, hi)))
+
+        h_codes = keep.tile([P, S], U32, name="h_codes", align_bytes=64)
+        h_scales = keep.tile([P, S], U8, name="h_scales", align_bytes=64)
+
+        def make_h(s):
+            grouped = stage.tile([P, BANK, PACK], BF16, name=f"h_bf{s}", tag="stage", align_bytes=64)
+            for c in range(BANK // P):
+                cols = slice(s * BANK + c * P, s * BANK + (c + 1) * P)
+                acc = psum_h.tile([P, PACK, P], F32, name="acc_h")
+                for t in range(PACK):
+                    for a in range(PASSES):
+                        nc.tensor.matmul_mx(
+                            out=acc[:, t, :],
+                            lhsT=down_codes[:, a, t * P : (t + 1) * P].bitcast(FP8X4),
+                            lhsT_scale=down_scales[:, a, t * P : (t + 1) * P],
+                            rhs=v_words[a][:, cols].bitcast(FP8X4),
+                            rhs_scale=v_scales[a][:, cols],
+                            start=(a == 0),
+                            stop=(a == PASSES - 1),
+                        )
+                nc.scalar.copy(out=grouped[:, c * P : (c + 1) * P, :], in_=acc[:].rearrange("p t n -> p n t"))
+            nc.vector.quantize_mx(
+                out=h_codes[:, s * BANK : (s + 1) * BANK].bitcast(FP8X4),
+                scales=h_scales[:, s * BANK : (s + 1) * BANK],
+                in_=grouped[:].rearrange("p n t -> p (n t)"),
+            )
+
+        up_codes = keep.tile([P, M], U32, name="up_codes", align_bytes=64)
+        up_scales = keep.tile([P, M], U8, name="up_scales", align_bytes=64)
+
+        def make_up(half):
+            cols = slice(half * BANK, (half + 1) * BANK)
+            grouped = stage.tile([P, PACK * BANK], BF16, name=f"up_bf{half}", tag="stage", align_bytes=64)
+            nc.scalar.copy(
+                out=grouped[:].rearrange("p (c j i) -> p c i j", j=4, i=PACK),
+                in_=up_raw[:, :, cols].rearrange("p i (c j) -> p c i j", j=4),
+            )
+            nc.vector.quantize_mx(out=up_codes[:, cols].bitcast(FP8X4), scales=up_scales[:, cols], in_=grouped[:])
+
+        make_h(0)
+        make_up(0)
+        make_h(1)
+        make_h(2)
+        make_up(1)
+
+        products = []
+        for b in range(BLOCKS):
+            result = picked.tile([P, S], F32, name=f"product{b}", tag="product", align_bytes=64)
+            products.append(result)
+            for s in range(SLICES):
+                cols = slice(s * BANK, (s + 1) * BANK)
+                acc = psum_y.tile([P, BANK], F32, name="acc_y")
+                for a in range(PASSES):
+                    nc.tensor.matmul_mx(
+                        out=acc[:],
+                        lhsT=w4[:, a, :].bitcast(U8)[:, 2 * P * b : 2 * P * (b + 1)].bitcast(FP4X4),
+                        lhsT_scale=w4_planes[:, a, :].bitcast(U8)[:, P * b : P * (b + 1)],
+                        rhs=v_words[a][:, cols].bitcast(FP8X4),
+                        rhs_scale=v_scales[a][:, cols],
+                        start=(a == 0),
+                        stop=False,
+                    )
+                nc.tensor.matmul_mx(
+                    out=acc[:],
+                    lhsT=up_codes[:, P * b : P * (b + 1)].bitcast(FP8X4),
+                    lhsT_scale=up_scales[:, P * b : P * (b + 1)],
+                    rhs=h_codes[:, cols].bitcast(FP8X4),
+                    rhs_scale=h_scales[:, cols],
+                    start=False,
+                    stop=True,
+                )
+                nc.scalar.copy(out=result[:, cols], in_=acc[:])
+
+        results = [keep.tile([P, S], F32, name=f"result{b}", align_bytes=64) for b in range(BLOCKS)]
+        pieces = [(b, 0, S) for b in range(BLOCKS - 1)]
+        pieces += [(BLOCKS - 1, s * BANK, (s + 1) * BANK) for s in range(SLICES)]
+
+        def gather(b, lo, hi):
+            nc.vector.tensor_copy(results[b][:, lo:hi], residual[b][:].indirect(listed(lo, hi)))
+
+        def finish(b, lo, hi):
+            nc.vector.tensor_tensor(results[b][:, lo:hi], results[b][:, lo:hi], products[b][:, lo:hi], ADD)
+            nc.sync.dma_start(out=out[b * P : (b + 1) * P, lo:hi], in_=results[b][:, lo:hi])
+
+        gather(*pieces[0])
+        for previous, piece in zip(pieces, pieces[1:]):
+            gather(*piece)
+            finish(*previous)
+        finish(*pieces[-1])

@@ -23,7 +23,7 @@ BANK = 512
 SLICES = S // BANK
 BLOCKS = M // P
 GROUP = 16
-STREAM_BUFS = 7
+STREAM_BUFS = 6
 STAGE_BUFS = 4
 
 
@@ -45,18 +45,21 @@ def tile_list_tabres_none_kernel(
         def listed(lo, hi):
             return offsets[:, lo // GROUP : hi // GROUP]
 
-        tab_planes = keep.tile([P, PASSES, T // 4], I32, name="tab_planes", align_bytes=64)
+        tab_planes = keep.tile([P, T // 4], I32, name="tab_planes", align_bytes=64)
         w4_planes = keep.tile([P, PASSES, M // 4], I32, name="w4_planes", align_bytes=64)
         nc.vector.memset(tab_planes[:], 0)
         nc.vector.memset(w4_planes[:], 0)
+        moved = keep.tile([P, S // 4], I32, name="moved", align_bytes=64)
+        nc.vector.memset(moved[:], 0)
 
         def load_planes(engine, planes, scales):
             rows = scales.bitcast(I32).rearrange("a (q r) c -> r q a c", r=4)
             for r in range(4):
                 engine.dma_start(out=planes[r:P:32, :, :], in_=rows[r])
 
-        load_planes(nc.scalar, tab_planes, tab_scales)
-        load_planes(nc.scalar, w4_planes, w4_scales)
+        tab_rows = tab_scales.bitcast(I32).rearrange("a (q r) c -> r q a c", r=4)
+        for r in range(4):
+            nc.scalar.dma_start(out=tab_planes[r:P:16, :], in_=tab_rows[r])
 
         def load_table(a):
             words = stream.tile([P, T], I32, name=f"tab{a}", tag="stream", align_bytes=64)
@@ -71,20 +74,28 @@ def tile_list_tabres_none_kernel(
             )
         tab0 = load_table(0)
         tab1 = load_table(1)
-        up_raw = stream.tile([P, PACK, M], F32, name="up_raw", tag="stream", align_bytes=64)
-        nc.sync.dma_start(out=up_raw[:], in_=up.rearrange("(p i) n -> p i n", i=PACK))
-        w4 = keep.tile([P, PASSES, 2 * M // 4], I32, name="w4", align_bytes=64)
-        nc.sync.dma_start(out=w4[:], in_=w4_words.bitcast(I32).rearrange("a p c -> p a c"))
         residual = []
-        for b in range(BLOCKS):
+
+        def load_residual(b):
             rows = stream.tile([P, T], F32, name=f"residual{b}", tag="stream", align_bytes=64)
             nc.sync.dma_start(out=rows[:], in_=rT[b * P : (b + 1) * P, :])
             residual.append(rows)
 
+        load_residual(0)
+        up_raw = stream.tile([P, PACK, M], F32, name="up_raw", tag="stream", align_bytes=64)
+        nc.sync.dma_start(out=up_raw[:], in_=up.rearrange("(p i) n -> p i n", i=PACK))
+        w4 = keep.tile([P, PASSES, 2 * M // 4], I32, name="w4", align_bytes=64)
+        nc.sync.dma_start(out=w4[:], in_=w4_words.bitcast(I32).rearrange("a p c -> p a c"))
+        load_planes(nc.sync, w4_planes, w4_scales)
+        for b in range(1, BLOCKS):
+            load_residual(b)
+
         v_words = [keep.tile([P, S], U32, name=f"v_words{a}", align_bytes=64) for a in range(PASSES)]
-        v_scales = [keep.tile([P, S], U8, name=f"v_scales{a}", align_bytes=64) for a in range(PASSES)]
-        for a in range(PASSES):
-            nc.vector.tensor_copy(v_scales[a][:], tab_planes[:, a, :].bitcast(U8).indirect(offsets[:]))
+        both = keep.tile([P, S], U8, name="both", align_bytes=64)
+        nc.vector.tensor_copy(both[:], tab_planes[:].bitcast(U8).indirect(offsets[:]))
+        for r in range(4):
+            nc.scalar.dma_start(out=moved[r:P:32, :], in_=both[16 + r : P : 32, :].bitcast(I32))
+        v_scales = [both[:], moved[:].bitcast(U8)]
         nc.vector.tensor_copy(v_words[0][:], tab0[:].bitcast(U32).indirect(offsets[:]))
 
         down_codes = keep.tile([P, PASSES, R], U32, name="down_codes", align_bytes=64)
@@ -149,8 +160,9 @@ def tile_list_tabres_none_kernel(
 
         products = []
         for b in range(BLOCKS):
-            result = picked.tile([P, S], F32, name=f"product{b}", tag="product", align_bytes=64)
-            products.append(result)
+            if b % 2 == 0:
+                products.append(picked.tile([P, 2 * S], F32, name=f"product{b}", tag="product", align_bytes=64))
+            result = products[b // 2][:, (b % 2) * S : (b % 2 + 1) * S]
             for s in range(SLICES):
                 cols = slice(s * BANK, (s + 1) * BANK)
                 acc = psum_y.tile([P, BANK], F32, name="acc_y")
@@ -175,17 +187,29 @@ def tile_list_tabres_none_kernel(
                 )
                 nc.scalar.copy(out=result[:, cols], in_=acc[:])
 
-        results = [keep.tile([P, S], F32, name=f"result{b}", align_bytes=64) for b in range(BLOCKS)]
-        pieces = [(b, 0, S) for b in range(BLOCKS - 1)]
-        pieces += [(BLOCKS - 1, s * BANK, (s + 1) * BANK) for s in range(SLICES)]
+        results = [keep.tile([P, 2 * S], F32, name=f"result{b}", align_bytes=64) for b in range(BLOCKS // 2)]
 
         def gather(b, lo, hi):
-            nc.vector.tensor_copy(results[b][:, lo:hi], residual[b][:].indirect(listed(lo, hi)))
+            base = (b % 2) * S
+            nc.vector.tensor_copy(results[b // 2][:, base + lo : base + hi], residual[b][:].indirect(listed(lo, hi)))
+
+        def add(pair, lo, hi):
+            nc.vector.tensor_tensor(results[pair][:, lo:hi], results[pair][:, lo:hi], products[pair][:, lo:hi], ADD)
 
         def finish(b, lo, hi):
-            nc.vector.tensor_tensor(results[b][:, lo:hi], results[b][:, lo:hi], products[b][:, lo:hi], ADD)
-            nc.sync.dma_start(out=out[b * P : (b + 1) * P, lo:hi], in_=results[b][:, lo:hi])
+            base = (b % 2) * S
+            add(b // 2, base + lo, base + hi)
+            nc.sync.dma_start(out=out[b * P : (b + 1) * P, lo:hi], in_=results[b // 2][:, base + lo : base + hi])
 
+        for pair in range(BLOCKS // 2 - 1):
+            gather(2 * pair, 0, S)
+            gather(2 * pair + 1, 0, S)
+            add(pair, 0, 2 * S)
+            nc.sync.dma_start(
+                out=out[2 * pair * P : 2 * (pair + 1) * P, :].rearrange("(b p) s -> p b s", p=P),
+                in_=results[pair][:].rearrange("p (b s) -> p b s", b=2),
+            )
+        pieces = [(BLOCKS - 2, 0, S)] + [(BLOCKS - 1, s * BANK, (s + 1) * BANK) for s in range(SLICES)]
         gather(*pieces[0])
         for previous, piece in zip(pieces, pieces[1:]):
             gather(*piece)

@@ -57,23 +57,17 @@ def tile_list_tabres_none_kernel(
             for r in range(4):
                 engine.dma_start(out=planes[r:P:32, :, :], in_=rows[r])
 
+        w4 = keep.tile([P, PASSES, 2 * M // 4], I32, name="w4", align_bytes=64)
+        nc.sync.dma_start(out=w4[:], in_=w4_words.bitcast(I32).rearrange("a p c -> p a c"))
         tab_rows = tab_scales.bitcast(I32).rearrange("a (q r) c -> r q a c", r=4)
         for r in range(4):
-            nc.scalar.dma_start(out=tab_planes[r:P:16, :], in_=tab_rows[r])
+            nc.sync.dma_start(out=tab_planes[r:P:16, :], in_=tab_rows[r])
 
         def load_table(a):
             words = stream.tile([P, T], I32, name=f"tab{a}", tag="stream", align_bytes=64)
             nc.sync.dma_start(out=words[:], in_=tab_words[a].rearrange("p t i -> p (t i)").bitcast(I32))
             return words
 
-        down_raw = stream.tile([P, PASSES, PACK, R], F32, name="down_raw", tag="stream", align_bytes=64)
-        for a in range(PASSES):
-            nc.sync.dma_start(
-                out=down_raw[:, a, :, :],
-                in_=down[a * K_PASS : (a + 1) * K_PASS, :].rearrange("(p i) r -> p i r", i=PACK),
-            )
-        tab0 = load_table(0)
-        tab1 = load_table(1)
         residual = []
 
         def load_residual(b):
@@ -81,13 +75,27 @@ def tile_list_tabres_none_kernel(
             nc.sync.dma_start(out=rows[:], in_=rT[b * P : (b + 1) * P, :])
             residual.append(rows)
 
+        def load_up(half):
+            nc.sync.dma_start(
+                out=up_raw[:, half, :, :],
+                in_=up[:, half * BANK : (half + 1) * BANK].rearrange("(p i) n -> p i n", i=PACK),
+            )
+
+        tab0 = load_table(0)
+        down_raw = stream.tile([P, PASSES, PACK, R], F32, name="down_raw", tag="stream", align_bytes=64)
+        for a in range(PASSES):
+            nc.sync.dma_start(
+                out=down_raw[:, a, :, :],
+                in_=down[a * K_PASS : (a + 1) * K_PASS, :].rearrange("(p i) r -> p i r", i=PACK),
+            )
+        tab1 = load_table(1)
         load_residual(0)
-        up_raw = stream.tile([P, PACK, M], F32, name="up_raw", tag="stream", align_bytes=64)
-        nc.sync.dma_start(out=up_raw[:], in_=up.rearrange("(p i) n -> p i n", i=PACK))
-        w4 = keep.tile([P, PASSES, 2 * M // 4], I32, name="w4", align_bytes=64)
-        nc.sync.dma_start(out=w4[:], in_=w4_words.bitcast(I32).rearrange("a p c -> p a c"))
         load_planes(nc.sync, w4_planes, w4_scales)
-        for b in range(1, BLOCKS):
+        up_raw = stream.tile([P, 2, PACK, BANK], F32, name="up_raw", tag="stream", align_bytes=64)
+        load_up(0)
+        load_residual(1)
+        load_up(1)
+        for b in range(2, BLOCKS):
             load_residual(b)
 
         v_words = [keep.tile([P, S], U32, name=f"v_words{a}", align_bytes=64) for a in range(PASSES)]
@@ -148,7 +156,7 @@ def tile_list_tabres_none_kernel(
             grouped = stage.tile([P, PACK * BANK], BF16, name=f"up_bf{half}", tag="stage", align_bytes=64)
             nc.scalar.copy(
                 out=grouped[:].rearrange("p (c j i) -> p c i j", j=4, i=PACK),
-                in_=up_raw[:, :, cols].rearrange("p i (c j) -> p c i j", j=4),
+                in_=up_raw[:, half, :, :].rearrange("p i (c j) -> p c i j", j=4),
             )
             nc.vector.quantize_mx(out=up_codes[:, cols].bitcast(FP8X4), scales=up_scales[:, cols], in_=grouped[:])
 

@@ -35,7 +35,7 @@ def tile_list_tabres_none_kernel(
         keep = ctx.enter_context(tc.tile_pool(name="keep", bufs=1))
         stream = ctx.enter_context(tc.tile_pool(name="stream", bufs=STREAM_BUFS))
         stage = ctx.enter_context(tc.tile_pool(name="stage", bufs=STAGE_BUFS))
-        picked = ctx.enter_context(tc.tile_pool(name="picked", bufs=2))
+        picked = ctx.enter_context(tc.tile_pool(name="picked", bufs=4))
         psum_h = ctx.enter_context(tc.psum_pool(name="psum_h", bufs=3))
         psum_y = ctx.enter_context(tc.psum_pool(name="psum_y", bufs=5))
 
@@ -167,10 +167,10 @@ def tile_list_tabres_none_kernel(
         make_up(1)
 
         products = []
+        last_banks = []
         for b in range(BLOCKS):
-            if b % 2 == 0:
-                products.append(picked.tile([P, 2 * S], F32, name=f"product{b}", tag="product", align_bytes=64))
-            result = products[b // 2][:, (b % 2) * S : (b % 2 + 1) * S]
+            if b < BLOCKS - 1:
+                products.append(picked.tile([P, S], F32, name=f"product{b}", tag="product", align_bytes=64))
             for s in range(SLICES):
                 cols = slice(s * BANK, (s + 1) * BANK)
                 acc = psum_y.tile([P, BANK], F32, name="acc_y")
@@ -193,33 +193,28 @@ def tile_list_tabres_none_kernel(
                     start=False,
                     stop=True,
                 )
-                nc.scalar.copy(out=result[:, cols], in_=acc[:])
+                if b < BLOCKS - 1:
+                    nc.scalar.copy(out=products[b][:, cols], in_=acc[:])
+                else:
+                    last_banks.append(acc)
 
-        results = [keep.tile([P, 2 * S], F32, name=f"result{b}", align_bytes=64) for b in range(BLOCKS // 2)]
+        results = [keep.tile([P, S], F32, name=f"result{b}", align_bytes=64) for b in range(BLOCKS)]
 
         def gather(b, lo, hi):
-            base = (b % 2) * S
-            nc.vector.tensor_copy(results[b // 2][:, base + lo : base + hi], residual[b][:].indirect(listed(lo, hi)))
+            nc.vector.tensor_copy(results[b][:, lo:hi], residual[b][:].indirect(listed(lo, hi)))
 
-        def add(pair, lo, hi):
-            nc.vector.tensor_tensor(results[pair][:, lo:hi], results[pair][:, lo:hi], products[pair][:, lo:hi], ADD)
+        def store(b, lo, hi):
+            nc.sync.dma_start(out=out[b * P : (b + 1) * P, lo:hi], in_=results[b][:, lo:hi])
 
-        def finish(b, lo, hi):
-            base = (b % 2) * S
-            add(b // 2, base + lo, base + hi)
-            nc.sync.dma_start(out=out[b * P : (b + 1) * P, lo:hi], in_=results[b // 2][:, base + lo : base + hi])
-
-        for pair in range(BLOCKS // 2 - 1):
-            gather(2 * pair, 0, S)
-            gather(2 * pair + 1, 0, S)
-            add(pair, 0, 2 * S)
-            nc.sync.dma_start(
-                out=out[2 * pair * P : 2 * (pair + 1) * P, :].rearrange("(b p) s -> p b s", p=P),
-                in_=results[pair][:].rearrange("p (b s) -> p b s", b=2),
-            )
-        pieces = [(BLOCKS - 2, 0, S)] + [(BLOCKS - 1, s * BANK, (s + 1) * BANK) for s in range(SLICES)]
-        gather(*pieces[0])
-        for previous, piece in zip(pieces, pieces[1:]):
-            gather(*piece)
-            finish(*previous)
-        finish(*pieces[-1])
+        for b in range(BLOCKS - 1):
+            gather(b, 0, S)
+            nc.gpsimd.tensor_tensor(results[b][:], results[b][:], products[b][:], ADD)
+            store(b, 0, S)
+        last = BLOCKS - 1
+        for s in range(SLICES + 1):
+            if s < SLICES:
+                gather(last, s * BANK, (s + 1) * BANK)
+            if s > 0:
+                lo, hi = (s - 1) * BANK, s * BANK
+                nc.vector.tensor_tensor(results[last][:, lo:hi], last_banks[s - 1][:], results[last][:, lo:hi], ADD)
+                store(last, lo, hi)

@@ -49,7 +49,7 @@ def tile_list_tabres_none_kernel(
         w4_planes = keep.tile([P, PASSES, M // 4], I32, name="w4_planes", align_bytes=64)
         nc.vector.memset(tab_planes[:], 0)
         nc.vector.memset(w4_planes[:], 0)
-        moved = keep.tile([P, S // 4], I32, name="moved", align_bytes=64)
+        moved = keep.tile([P, PASSES, S // 4], I32, name="moved", align_bytes=64)
         nc.vector.memset(moved[:], 0)
 
         def load_planes(engine, planes, scales):
@@ -59,9 +59,8 @@ def tile_list_tabres_none_kernel(
 
         w4 = keep.tile([P, PASSES, 2 * M // 4], I32, name="w4", align_bytes=64)
         nc.sync.dma_start(out=w4[:], in_=w4_words.bitcast(I32).rearrange("a p c -> p a c"))
-        tab_rows = tab_scales.bitcast(I32).rearrange("a (q r) c -> r q a c", r=4)
-        for r in range(4):
-            nc.sync.dma_start(out=tab_planes[r:P:16, :], in_=tab_rows[r])
+        nc.sync.dma_start(out=tab_planes[0:P:4, :], in_=tab_scales.bitcast(I32).rearrange("a q c -> (a q) c"))
+        load_planes(nc.gpsimd, w4_planes, w4_scales)
 
         def load_table(a):
             words = stream.tile([P, T], I32, name=f"tab{a}", tag="stream", align_bytes=64)
@@ -75,12 +74,6 @@ def tile_list_tabres_none_kernel(
             nc.sync.dma_start(out=rows[:], in_=rT[b * P : (b + 1) * P, :])
             residual.append(rows)
 
-        def load_up(half):
-            nc.sync.dma_start(
-                out=up_raw[:, half, :, :],
-                in_=up[:, half * BANK : (half + 1) * BANK].rearrange("(p i) n -> p i n", i=PACK),
-            )
-
         tab0 = load_table(0)
         down_raw = stream.tile([P, PASSES, PACK, R], F32, name="down_raw", tag="stream", align_bytes=64)
         for a in range(PASSES):
@@ -89,21 +82,20 @@ def tile_list_tabres_none_kernel(
                 in_=down[a * K_PASS : (a + 1) * K_PASS, :].rearrange("(p i) r -> p i r", i=PACK),
             )
         tab1 = load_table(1)
-        load_residual(0)
-        load_planes(nc.sync, w4_planes, w4_scales)
-        up_raw = stream.tile([P, 2, PACK, BANK], F32, name="up_raw", tag="stream", align_bytes=64)
-        load_up(0)
-        load_residual(1)
-        load_up(1)
-        for b in range(2, BLOCKS):
+        up_raw = stream.tile([P, PACK, M], F32, name="up_raw", tag="stream", align_bytes=64)
+        nc.sync.dma_start(out=up_raw[:], in_=up.rearrange("(p i) n -> p i n", i=PACK))
+        for b in range(BLOCKS):
             load_residual(b)
 
         v_words = [keep.tile([P, S], U32, name=f"v_words{a}", align_bytes=64) for a in range(PASSES)]
         both = keep.tile([P, S], U8, name="both", align_bytes=64)
         nc.vector.tensor_copy(both[:], tab_planes[:].bitcast(U8).indirect(offsets[:]))
-        for r in range(4):
-            nc.scalar.dma_start(out=moved[r:P:32, :], in_=both[16 + r : P : 32, :].bitcast(I32))
-        v_scales = [both[:], moved[:].bitcast(U8)]
+        for a in range(PASSES):
+            for r in range(4):
+                (nc.scalar, nc.gpsimd)[a].dma_start(
+                    out=moved[r:P:32, a, :], in_=both[64 * a + 4 * r : 64 * (a + 1) : 16, :].bitcast(I32)
+                )
+        v_scales = [moved[:, a, :].bitcast(U8) for a in range(PASSES)]
         nc.vector.tensor_copy(v_words[0][:], tab0[:].bitcast(U32).indirect(offsets[:]))
 
         down_codes = keep.tile([P, PASSES, R], U32, name="down_codes", align_bytes=64)
@@ -156,7 +148,7 @@ def tile_list_tabres_none_kernel(
             grouped = stage.tile([P, PACK * BANK], BF16, name=f"up_bf{half}", tag="stage", align_bytes=64)
             nc.scalar.copy(
                 out=grouped[:].rearrange("p (c j i) -> p c i j", j=4, i=PACK),
-                in_=up_raw[:, half, :, :].rearrange("p i (c j) -> p c i j", j=4),
+                in_=up_raw[:, :, cols].rearrange("p i (c j) -> p c i j", j=4),
             )
             nc.vector.quantize_mx(out=up_codes[:, cols].bitcast(FP8X4), scales=up_scales[:, cols], in_=grouped[:])
 
@@ -217,4 +209,4 @@ def tile_list_tabres_none_kernel(
             if s > 0:
                 lo, hi = (s - 1) * BANK, s * BANK
                 nc.vector.tensor_tensor(results[last][:, lo:hi], last_banks[s - 1][:], results[last][:, lo:hi], ADD)
-                store(last, lo, hi)
+        store(last, 0, S)

@@ -59,7 +59,6 @@ def tile_list_tabres_none_kernel(
 
         w4 = keep.tile([P, PASSES, 2 * M // 4], I32, name="w4", align_bytes=64)
         nc.sync.dma_start(out=w4[:], in_=w4_words.bitcast(I32).rearrange("a p c -> p a c"))
-        nc.sync.dma_start(out=tab_planes[0:P:4, :], in_=tab_scales.bitcast(I32).rearrange("a q c -> (a q) c"))
         load_planes(nc.gpsimd, w4_planes, w4_scales)
 
         def load_table(a):
@@ -74,13 +73,18 @@ def tile_list_tabres_none_kernel(
             nc.sync.dma_start(out=rows[:], in_=rT[b * P : (b + 1) * P, :])
             residual.append(rows)
 
-        tab0 = load_table(0)
         down_raw = stream.tile([P, PASSES, PACK, R], F32, name="down_raw", tag="stream", align_bytes=64)
-        for a in range(PASSES):
+
+        def load_down(a):
             nc.sync.dma_start(
                 out=down_raw[:, a, :, :],
                 in_=down[a * K_PASS : (a + 1) * K_PASS, :].rearrange("(p i) r -> p i r", i=PACK),
             )
+
+        load_down(0)
+        nc.sync.dma_start(out=tab_planes[0:P:4, :], in_=tab_scales.bitcast(I32).rearrange("a q c -> (a q) c"))
+        tab0 = load_table(0)
+        load_down(1)
         tab1 = load_table(1)
         up_raw = stream.tile([P, PACK, M], F32, name="up_raw", tag="stream", align_bytes=64)
         nc.sync.dma_start(out=up_raw[:], in_=up.rearrange("(p i) n -> p i n", i=PACK))
@@ -146,17 +150,16 @@ def tile_list_tabres_none_kernel(
         def make_up(half):
             cols = slice(half * BANK, (half + 1) * BANK)
             grouped = stage.tile([P, PACK * BANK], BF16, name=f"up_bf{half}", tag="stage", align_bytes=64)
-            nc.scalar.copy(
+            nc.vector.tensor_copy(
                 out=grouped[:].rearrange("p (c j i) -> p c i j", j=4, i=PACK),
                 in_=up_raw[:, :, cols].rearrange("p i (c j) -> p c i j", j=4),
             )
             nc.vector.quantize_mx(out=up_codes[:, cols].bitcast(FP8X4), scales=up_scales[:, cols], in_=grouped[:])
 
-        make_h(0)
         make_up(0)
-        make_h(1)
-        make_h(2)
         make_up(1)
+        for s in range(SLICES):
+            make_h(s)
 
         products = []
         last_banks = []
@@ -166,6 +169,15 @@ def tile_list_tabres_none_kernel(
             for s in range(SLICES):
                 cols = slice(s * BANK, (s + 1) * BANK)
                 acc = psum_y.tile([P, BANK], F32, name="acc_y")
+                nc.tensor.matmul_mx(
+                    out=acc[:],
+                    lhsT=up_codes[:, P * b : P * (b + 1)].bitcast(FP8X4),
+                    lhsT_scale=up_scales[:, P * b : P * (b + 1)],
+                    rhs=h_codes[:, cols].bitcast(FP8X4),
+                    rhs_scale=h_scales[:, cols],
+                    start=True,
+                    stop=False,
+                )
                 for a in range(PASSES):
                     nc.tensor.matmul_mx(
                         out=acc[:],
@@ -173,18 +185,9 @@ def tile_list_tabres_none_kernel(
                         lhsT_scale=w4_planes[:, a, :].bitcast(U8)[:, P * b : P * (b + 1)],
                         rhs=v_words[a][:, cols].bitcast(FP8X4),
                         rhs_scale=v_scales[a][:, cols],
-                        start=(a == 0),
-                        stop=False,
+                        start=False,
+                        stop=(a == PASSES - 1),
                     )
-                nc.tensor.matmul_mx(
-                    out=acc[:],
-                    lhsT=up_codes[:, P * b : P * (b + 1)].bitcast(FP8X4),
-                    lhsT_scale=up_scales[:, P * b : P * (b + 1)],
-                    rhs=h_codes[:, cols].bitcast(FP8X4),
-                    rhs_scale=h_scales[:, cols],
-                    start=False,
-                    stop=True,
-                )
                 if b < BLOCKS - 1:
                     nc.scalar.copy(out=products[b][:, cols], in_=acc[:])
                 else:

@@ -23,8 +23,9 @@ BANK = 512
 SLICES = S // BANK
 BLOCKS = M // P
 GROUP = 16
-STREAM_BUFS = 6
-STAGE_BUFS = 4
+SLOT = 4 * T
+EARLY = 3
+STAGE_BUFS = 3
 
 
 def tile_list_tabres_none_kernel(
@@ -33,9 +34,8 @@ def tile_list_tabres_none_kernel(
     nc = tc.nc
     with ExitStack() as ctx:
         keep = ctx.enter_context(tc.tile_pool(name="keep", bufs=1))
-        stream = ctx.enter_context(tc.tile_pool(name="stream", bufs=STREAM_BUFS))
+        stream = ctx.enter_context(tc.tile_pool(name="stream", bufs=1))
         stage = ctx.enter_context(tc.tile_pool(name="stage", bufs=STAGE_BUFS))
-        picked = ctx.enter_context(tc.tile_pool(name="picked", bufs=4))
         psum_h = ctx.enter_context(tc.psum_pool(name="psum_h", bufs=3))
         psum_y = ctx.enter_context(tc.psum_pool(name="psum_y", bufs=5))
 
@@ -46,34 +46,36 @@ def tile_list_tabres_none_kernel(
             return offsets[:, lo // GROUP : hi // GROUP]
 
         tab_planes = keep.tile([P, T // 4], I32, name="tab_planes", align_bytes=64)
-        w4_planes = keep.tile([P, PASSES, M // 4], I32, name="w4_planes", align_bytes=64)
+        w4_planes = keep.tile([P, PASSES, EARLY * P // 4], I32, name="w4_planes", align_bytes=64)
         nc.vector.memset(tab_planes[:], 0)
         nc.vector.memset(w4_planes[:], 0)
         moved = keep.tile([P, PASSES, S // 4], I32, name="moved", align_bytes=64)
         nc.vector.memset(moved[:], 0)
 
-        def load_planes(engine, planes, scales):
-            rows = scales.bitcast(I32).rearrange("a (q r) c -> r q a c", r=4)
+        def load_planes(engine, planes, lo, hi):
+            rows = w4_scales.bitcast(I32).rearrange("a (q r) c -> r q a c", r=4)
             for r in range(4):
-                engine.dma_start(out=planes[r:P:32, :, :], in_=rows[r])
+                engine.dma_start(out=planes[r:P:32, :, :], in_=rows[r][:, :, lo // 4 : hi // 4])
 
         w4 = keep.tile([P, PASSES, 2 * M // 4], I32, name="w4", align_bytes=64)
         nc.sync.dma_start(out=w4[:], in_=w4_words.bitcast(I32).rearrange("a p c -> p a c"))
-        load_planes(nc.gpsimd, w4_planes, w4_scales)
+        load_planes(nc.gpsimd, w4_planes, 0, EARLY * P)
 
         def load_table(a):
-            words = stream.tile([P, T], I32, name=f"tab{a}", tag="stream", align_bytes=64)
+            words = stream.tile([P, T], I32, name=f"tab{a}", offset=(1 + a) * SLOT, align_bytes=64)
             nc.sync.dma_start(out=words[:], in_=tab_words[a].rearrange("p t i -> p (t i)").bitcast(I32))
             return words
 
         residual = []
+        late_at = 7 * SLOT
+        places = [slot * SLOT for slot in (4, 1, 0, 2, 3, 5, 6, 4)]
 
         def load_residual(b):
-            rows = stream.tile([P, T], F32, name=f"residual{b}", tag="stream", align_bytes=64)
+            rows = stream.tile([P, T], F32, name=f"residual{b}", offset=places[b], align_bytes=64)
             nc.sync.dma_start(out=rows[:], in_=rT[b * P : (b + 1) * P, :])
             residual.append(rows)
 
-        down_raw = stream.tile([P, PASSES, PACK, R], F32, name="down_raw", tag="stream", align_bytes=64)
+        down_raw = stream.tile([P, PASSES, PACK, R], F32, name="down_raw", offset=0, align_bytes=64)
 
         def load_down(a):
             nc.sync.dma_start(
@@ -82,13 +84,14 @@ def tile_list_tabres_none_kernel(
             )
 
         load_down(0)
-        nc.sync.dma_start(out=tab_planes[0:P:4, :], in_=tab_scales.bitcast(I32).rearrange("a q c -> (a q) c"))
+        for a in range(PASSES):
+            nc.sync.dma_start(out=tab_planes[32 + a : 96 : 4, :], in_=tab_scales[a].bitcast(I32))
         tab0 = load_table(0)
         load_down(1)
         tab1 = load_table(1)
-        up_raw = stream.tile([P, PACK, M], F32, name="up_raw", tag="stream", align_bytes=64)
+        up_raw = stream.tile([P, PACK, M], F32, name="up_raw", offset=3 * SLOT, align_bytes=64)
         nc.sync.dma_start(out=up_raw[:], in_=up.rearrange("(p i) n -> p i n", i=PACK))
-        for b in range(BLOCKS):
+        for b in range(5):
             load_residual(b)
 
         v_words = [keep.tile([P, S], U32, name=f"v_words{a}", align_bytes=64) for a in range(PASSES)]
@@ -97,7 +100,7 @@ def tile_list_tabres_none_kernel(
         for a in range(PASSES):
             for r in range(4):
                 (nc.scalar, nc.gpsimd)[a].dma_start(
-                    out=moved[r:P:32, a, :], in_=both[64 * a + 4 * r : 64 * (a + 1) : 16, :].bitcast(I32)
+                    out=moved[r:P:32, a, :], in_=both[32 + a + 4 * r : 96 : 16, :].bitcast(I32)
                 )
         v_scales = [moved[:, a, :].bitcast(U8) for a in range(PASSES)]
         nc.vector.tensor_copy(v_words[0][:], tab0[:].bitcast(U32).indirect(offsets[:]))
@@ -161,38 +164,6 @@ def tile_list_tabres_none_kernel(
         for s in range(SLICES):
             make_h(s)
 
-        products = []
-        last_banks = []
-        for b in range(BLOCKS):
-            if b < BLOCKS - 1:
-                products.append(picked.tile([P, S], F32, name=f"product{b}", tag="product", align_bytes=64))
-            for s in range(SLICES):
-                cols = slice(s * BANK, (s + 1) * BANK)
-                acc = psum_y.tile([P, BANK], F32, name="acc_y")
-                nc.tensor.matmul_mx(
-                    out=acc[:],
-                    lhsT=up_codes[:, P * b : P * (b + 1)].bitcast(FP8X4),
-                    lhsT_scale=up_scales[:, P * b : P * (b + 1)],
-                    rhs=h_codes[:, cols].bitcast(FP8X4),
-                    rhs_scale=h_scales[:, cols],
-                    start=True,
-                    stop=False,
-                )
-                for a in range(PASSES):
-                    nc.tensor.matmul_mx(
-                        out=acc[:],
-                        lhsT=w4[:, a, :].bitcast(U8)[:, 2 * P * b : 2 * P * (b + 1)].bitcast(FP4X4),
-                        lhsT_scale=w4_planes[:, a, :].bitcast(U8)[:, P * b : P * (b + 1)],
-                        rhs=v_words[a][:, cols].bitcast(FP8X4),
-                        rhs_scale=v_scales[a][:, cols],
-                        start=False,
-                        stop=(a == PASSES - 1),
-                    )
-                if b < BLOCKS - 1:
-                    nc.scalar.copy(out=products[b][:, cols], in_=acc[:])
-                else:
-                    last_banks.append(acc)
-
         results = [keep.tile([P, S], F32, name=f"result{b}", align_bytes=64) for b in range(BLOCKS)]
 
         def gather(b, lo, hi):
@@ -201,15 +172,66 @@ def tile_list_tabres_none_kernel(
         def store(b, lo, hi):
             nc.sync.dma_start(out=out[b * P : (b + 1) * P, lo:hi], in_=results[b][:, lo:hi])
 
-        for b in range(BLOCKS - 1):
+        def make_y(b, s, planes, first):
+            cols = slice(s * BANK, (s + 1) * BANK)
+            acc = psum_y.tile([P, BANK], F32, name="acc_y")
+            nc.tensor.matmul_mx(
+                out=acc[:],
+                lhsT=up_codes[:, P * b : P * (b + 1)].bitcast(FP8X4),
+                lhsT_scale=up_scales[:, P * b : P * (b + 1)],
+                rhs=h_codes[:, cols].bitcast(FP8X4),
+                rhs_scale=h_scales[:, cols],
+                start=True,
+                stop=False,
+            )
+            for a in range(PASSES):
+                nc.tensor.matmul_mx(
+                    out=acc[:],
+                    lhsT=w4[:, a, :].bitcast(U8)[:, 2 * P * b : 2 * P * (b + 1)].bitcast(FP4X4),
+                    lhsT_scale=planes[:, a, :].bitcast(U8)[:, P * (b - first) : P * (b - first + 1)],
+                    rhs=v_words[a][:, cols].bitcast(FP8X4),
+                    rhs_scale=v_scales[a][:, cols],
+                    start=False,
+                    stop=(a == PASSES - 1),
+                )
+            return acc
+
+        def finish(b, product, planes, first):
+            for s in range(SLICES):
+                nc.scalar.copy(out=product[:, s * BANK : (s + 1) * BANK], in_=make_y(b, s, planes, first)[:])
             gather(b, 0, S)
-            nc.gpsimd.tensor_tensor(results[b][:], results[b][:], products[b][:], ADD)
+            nc.gpsimd.tensor_tensor(results[b][:], results[b][:], product[:], ADD)
             store(b, 0, S)
+
+        def staged(b, place):
+            return stream.tile([P, S], F32, name=f"product{b}", offset=place, align_bytes=64)
+
+        finish(0, staged(0, late_at), w4_planes, 0)
+        late_planes = stream.tile([P, PASSES, (M - EARLY * P) // 4], I32, name="late_planes", offset=late_at, align_bytes=64)
+        nc.gpsimd.memset(late_planes[:], 0)
+        load_planes(nc.sync, late_planes, EARLY * P, M)
+        gather(1, 0, S)
+        for s in range(SLICES):
+            cols = slice(s * BANK, (s + 1) * BANK)
+            place = (6 * SLOT - 2 * BANK, places[0], late_at + 4 * S)[s]
+            part = stream.tile([P, BANK], F32, name=f"part{s}", offset=place, align_bytes=64)
+            nc.scalar.copy(out=part[:], in_=make_y(1, s, w4_planes, 0)[:])
+            nc.gpsimd.tensor_tensor(results[1][:, cols], results[1][:, cols], part[:], ADD)
+        for b in range(5, BLOCKS):
+            load_residual(b)
+        store(1, 0, S)
         last = BLOCKS - 1
+        for b in range(2, last):
+            product = staged(b, places[1 + (b - 2) % 4] + (b - 2) // 4 * 4 * S)
+            if b < EARLY:
+                finish(b, product, w4_planes, 0)
+            else:
+                finish(b, product, late_planes, EARLY)
+        banks = [make_y(last, s, late_planes, EARLY) for s in range(SLICES)]
         for s in range(SLICES + 1):
             if s < SLICES:
                 gather(last, s * BANK, (s + 1) * BANK)
             if s > 0:
                 lo, hi = (s - 1) * BANK, s * BANK
-                nc.vector.tensor_tensor(results[last][:, lo:hi], last_banks[s - 1][:], results[last][:, lo:hi], ADD)
+                nc.vector.tensor_tensor(results[last][:, lo:hi], banks[s - 1][:], results[last][:, lo:hi], ADD)
         store(last, 0, S)

@@ -45,9 +45,10 @@ def tile_list_tabres_none_kernel(
         def listed(lo, hi):
             return offsets[:, lo // GROUP : hi // GROUP]
 
-        tab_planes = keep.tile([P, T // 4], I32, name="tab_planes", align_bytes=64)
+        tab_planes = [keep.tile([P, T // 4], I32, name=f"tab_planes{a}", align_bytes=64) for a in range(PASSES)]
         w4_planes = keep.tile([P, PASSES, EARLY * P // 4], I32, name="w4_planes", align_bytes=64)
-        nc.vector.memset(tab_planes[:], 0)
+        for planes in tab_planes:
+            nc.vector.memset(planes[:], 0)
         nc.vector.memset(w4_planes[:], 0)
         moved = keep.tile([P, PASSES, S // 4], I32, name="moved", align_bytes=64)
         nc.vector.memset(moved[:], 0)
@@ -68,7 +69,7 @@ def tile_list_tabres_none_kernel(
 
         residual = []
         late_at = 7 * SLOT
-        places = [slot * SLOT for slot in (4, 1, 0, 2, 3, 5, 6, 4)]
+        places = [slot * SLOT for slot in (0, 1, 2, 3, 4, 5, 6, 0)]
 
         def load_residual(b):
             rows = stream.tile([P, T], F32, name=f"residual{b}", offset=places[b], align_bytes=64)
@@ -85,23 +86,21 @@ def tile_list_tabres_none_kernel(
 
         load_down(0)
         for a in range(PASSES):
-            nc.sync.dma_start(out=tab_planes[32 + a : 96 : 4, :], in_=tab_scales[a].bitcast(I32))
+            nc.sync.dma_start(out=tab_planes[a][32:96:4, :], in_=tab_scales[a].bitcast(I32))
         tab0 = load_table(0)
         load_down(1)
         tab1 = load_table(1)
         up_raw = stream.tile([P, PACK, M], F32, name="up_raw", offset=3 * SLOT, align_bytes=64)
         nc.sync.dma_start(out=up_raw[:], in_=up.rearrange("(p i) n -> p i n", i=PACK))
-        for b in range(5):
+        for b in range(4):
             load_residual(b)
 
         v_words = [keep.tile([P, S], U32, name=f"v_words{a}", align_bytes=64) for a in range(PASSES)]
-        both = keep.tile([P, S], U8, name="both", align_bytes=64)
-        nc.vector.tensor_copy(both[:], tab_planes[:].bitcast(U8).indirect(offsets[:]))
+        both = keep.tile([P, PASSES, S], U8, name="both", align_bytes=64)
         for a in range(PASSES):
-            for r in range(4):
-                (nc.scalar, nc.gpsimd)[a].dma_start(
-                    out=moved[r:P:32, a, :], in_=both[32 + a + 4 * r : 96 : 16, :].bitcast(I32)
-                )
+            nc.vector.tensor_copy(both[:, a, :], tab_planes[a][:].bitcast(U8).indirect(offsets[:]))
+        for r in range(4):
+            nc.scalar.dma_start(out=moved[r:P:32, :, :], in_=both[32 + 4 * r : 96 : 16, :, :].bitcast(I32))
         v_scales = [moved[:, a, :].bitcast(U8) for a in range(PASSES)]
         nc.vector.tensor_copy(v_words[0][:], tab0[:].bitcast(U32).indirect(offsets[:]))
 
@@ -152,7 +151,9 @@ def tile_list_tabres_none_kernel(
 
         def make_up(half):
             cols = slice(half * BANK, (half + 1) * BANK)
-            grouped = stage.tile([P, PACK * BANK], BF16, name=f"up_bf{half}", tag="stage", align_bytes=64)
+            grouped = stream.tile(
+                [P, PACK * BANK], BF16, name=f"up_bf{half}", offset=4 * SLOT + half * 2 * PACK * BANK, align_bytes=64
+            )
             nc.vector.tensor_copy(
                 out=grouped[:].rearrange("p (c j i) -> p c i j", j=4, i=PACK),
                 in_=up_raw[:, :, cols].rearrange("p i (c j) -> p c i j", j=4),
@@ -161,6 +162,7 @@ def tile_list_tabres_none_kernel(
 
         make_up(0)
         make_up(1)
+        load_residual(4)
         for s in range(SLICES):
             make_h(s)
 

@@ -47,9 +47,9 @@ def tile_list_tabres_none_kernel(
 
         tab_planes = [keep.tile([P, T // 4], I32, name=f"tab_planes{a}", align_bytes=64) for a in range(PASSES)]
         w4_planes = keep.tile([P, PASSES, EARLY * P // 4], I32, name="w4_planes", align_bytes=64)
+        nc.vector.memset(w4_planes[:], 0)
         for planes in tab_planes:
             nc.vector.memset(planes[:], 0)
-        nc.vector.memset(w4_planes[:], 0)
         moved = keep.tile([P, PASSES, S // 4], I32, name="moved", align_bytes=64)
         nc.vector.memset(moved[:], 0)
 
@@ -60,7 +60,7 @@ def tile_list_tabres_none_kernel(
 
         w4 = keep.tile([P, PASSES, 2 * M // 4], I32, name="w4", align_bytes=64)
         nc.sync.dma_start(out=w4[:], in_=w4_words.bitcast(I32).rearrange("a p c -> p a c"))
-        load_planes(nc.gpsimd, w4_planes, 0, EARLY * P)
+        load_planes(nc.scalar, w4_planes, 0, EARLY * P)
 
         def load_table(a):
             words = stream.tile([P, T], I32, name=f"tab{a}", offset=(1 + a) * SLOT, align_bytes=64)

@@ -60,7 +60,7 @@ def tile_list_tabres_none_kernel(
 
         w4 = keep.tile([P, PASSES, 2 * M // 4], I32, name="w4", align_bytes=64)
         nc.sync.dma_start(out=w4[:], in_=w4_words.bitcast(I32).rearrange("a p c -> p a c"))
-        load_planes(nc.scalar, w4_planes, 0, EARLY * P)
+        load_planes(nc.sync, w4_planes, 0, EARLY * P)
 
         def load_table(a):
             words = stream.tile([P, T], I32, name=f"tab{a}", offset=(1 + a) * SLOT, align_bytes=64)

@@ -26,6 +26,7 @@ GROUP = 16
 SLOT = 4 * T
 EARLY = 3
 STAGE_BUFS = 3
+LINE = 256
 
 
 def tile_list_tabres_none_kernel(
@@ -45,12 +46,12 @@ def tile_list_tabres_none_kernel(
         def listed(lo, hi):
             return offsets[:, lo // GROUP : hi // GROUP]
 
-        tab_planes = [keep.tile([P, T // 4], I32, name=f"tab_planes{a}", align_bytes=64) for a in range(PASSES)]
-        w4_planes = keep.tile([P, PASSES, EARLY * P // 4], I32, name="w4_planes", align_bytes=64)
+        tab_planes = [keep.tile([P, T // 4], I32, name=f"tab_planes{a}", align_bytes=LINE) for a in range(PASSES)]
+        w4_planes = keep.tile([P, PASSES, EARLY * P // 4], I32, name="w4_planes", align_bytes=LINE)
         nc.vector.memset(w4_planes[:], 0)
         for planes in tab_planes:
             nc.vector.memset(planes[:], 0)
-        moved = keep.tile([P, PASSES, S // 4], I32, name="moved", align_bytes=64)
+        moved = keep.tile([P, PASSES, S // 4], I32, name="moved", align_bytes=LINE)
         nc.vector.memset(moved[:], 0)
 
         def load_planes(engine, planes, lo, hi):
@@ -58,12 +59,12 @@ def tile_list_tabres_none_kernel(
             for r in range(4):
                 engine.dma_start(out=planes[r:P:32, :, :], in_=rows[r][:, :, lo // 4 : hi // 4])
 
-        w4 = keep.tile([P, PASSES, 2 * M // 4], I32, name="w4", align_bytes=64)
+        w4 = keep.tile([P, PASSES, 2 * M // 4], I32, name="w4", align_bytes=LINE)
         nc.sync.dma_start(out=w4[:], in_=w4_words.bitcast(I32).rearrange("a p c -> p a c"))
         load_planes(nc.sync, w4_planes, 0, EARLY * P)
 
         def load_table(a):
-            words = stream.tile([P, T], I32, name=f"tab{a}", offset=(1 + a) * SLOT, align_bytes=64)
+            words = stream.tile([P, T], I32, name=f"tab{a}", offset=(1 + a) * SLOT, align_bytes=LINE)
             nc.sync.dma_start(out=words[:], in_=tab_words[a].rearrange("p t i -> p (t i)").bitcast(I32))
             return words
 
@@ -72,11 +73,11 @@ def tile_list_tabres_none_kernel(
         places = [slot * SLOT for slot in (0, 1, 2, 3, 4, 5, 6, 0)]
 
         def load_residual(b):
-            rows = stream.tile([P, T], F32, name=f"residual{b}", offset=places[b], align_bytes=64)
+            rows = stream.tile([P, T], F32, name=f"residual{b}", offset=places[b], align_bytes=LINE)
             nc.sync.dma_start(out=rows[:], in_=rT[b * P : (b + 1) * P, :])
             residual.append(rows)
 
-        down_raw = stream.tile([P, PASSES, PACK, R], F32, name="down_raw", offset=0, align_bytes=64)
+        down_raw = stream.tile([P, PASSES, PACK, R], F32, name="down_raw", offset=0, align_bytes=LINE)
 
         def load_down(a):
             nc.sync.dma_start(
@@ -90,13 +91,13 @@ def tile_list_tabres_none_kernel(
         tab0 = load_table(0)
         load_down(1)
         tab1 = load_table(1)
-        up_raw = stream.tile([P, PACK, M], F32, name="up_raw", offset=3 * SLOT, align_bytes=64)
+        up_raw = stream.tile([P, PACK, M], F32, name="up_raw", offset=3 * SLOT, align_bytes=LINE)
         nc.sync.dma_start(out=up_raw[:], in_=up.rearrange("(p i) n -> p i n", i=PACK))
         for b in range(4):
             load_residual(b)
 
-        v_words = [keep.tile([P, S], U32, name=f"v_words{a}", align_bytes=64) for a in range(PASSES)]
-        both = keep.tile([P, PASSES, S], U8, name="both", align_bytes=64)
+        v_words = [keep.tile([P, S], U32, name=f"v_words{a}", align_bytes=LINE) for a in range(PASSES)]
+        both = keep.tile([P, PASSES, S], U8, name="both", align_bytes=LINE)
         for a in range(PASSES):
             nc.vector.tensor_copy(both[:, a, :], tab_planes[a][:].bitcast(U8).indirect(offsets[:]))
         for r in range(4):
@@ -104,10 +105,10 @@ def tile_list_tabres_none_kernel(
         v_scales = [moved[:, a, :].bitcast(U8) for a in range(PASSES)]
         nc.vector.tensor_copy(v_words[0][:], tab0[:].bitcast(U32).indirect(offsets[:]))
 
-        down_codes = keep.tile([P, PASSES, R], U32, name="down_codes", align_bytes=64)
-        down_scales = keep.tile([P, PASSES, R], U8, name="down_scales", align_bytes=64)
+        down_codes = keep.tile([P, PASSES, R], U32, name="down_codes", align_bytes=LINE)
+        down_scales = keep.tile([P, PASSES, R], U8, name="down_scales", align_bytes=LINE)
         for a in range(PASSES):
-            grouped = stage.tile([P, PACK * R], BF16, name=f"down_bf{a}", tag="stage", align_bytes=64)
+            grouped = stage.tile([P, PACK * R], BF16, name=f"down_bf{a}", tag="stage", align_bytes=LINE)
             nc.scalar.copy(
                 out=grouped[:].rearrange("p (t m i) -> p m t i", t=PACK, i=PACK),
                 in_=down_raw[:, a, :, :].rearrange("p i (m t) -> p m t i", t=PACK),
@@ -120,11 +121,11 @@ def tile_list_tabres_none_kernel(
             lo, hi = s * BANK, (s + 1) * BANK
             nc.vector.tensor_copy(v_words[1][:, lo:hi], tab1[:].bitcast(U32).indirect(listed(lo, hi)))
 
-        h_codes = keep.tile([P, S], U32, name="h_codes", align_bytes=64)
-        h_scales = keep.tile([P, S], U8, name="h_scales", align_bytes=64)
+        h_codes = keep.tile([P, S], U32, name="h_codes", align_bytes=LINE)
+        h_scales = keep.tile([P, S], U8, name="h_scales", align_bytes=LINE)
 
         def make_h(s):
-            grouped = stage.tile([P, BANK, PACK], BF16, name=f"h_bf{s}", tag="stage", align_bytes=64)
+            grouped = stage.tile([P, BANK, PACK], BF16, name=f"h_bf{s}", tag="stage", align_bytes=LINE)
             for c in range(BANK // P):
                 cols = slice(s * BANK + c * P, s * BANK + (c + 1) * P)
                 acc = psum_h.tile([P, PACK, P], F32, name="acc_h")
@@ -146,13 +147,13 @@ def tile_list_tabres_none_kernel(
                 in_=grouped[:].rearrange("p n t -> p (n t)"),
             )
 
-        up_codes = keep.tile([P, M], U32, name="up_codes", align_bytes=64)
-        up_scales = keep.tile([P, M], U8, name="up_scales", align_bytes=64)
+        up_codes = keep.tile([P, M], U32, name="up_codes", align_bytes=LINE)
+        up_scales = keep.tile([P, M], U8, name="up_scales", align_bytes=LINE)
 
         def make_up(half):
             cols = slice(half * BANK, (half + 1) * BANK)
             grouped = stream.tile(
-                [P, PACK * BANK], BF16, name=f"up_bf{half}", offset=4 * SLOT + half * 2 * PACK * BANK, align_bytes=64
+                [P, PACK * BANK], BF16, name=f"up_bf{half}", offset=4 * SLOT + half * 2 * PACK * BANK, align_bytes=LINE
             )
             nc.vector.tensor_copy(
                 out=grouped[:].rearrange("p (c j i) -> p c i j", j=4, i=PACK),
@@ -166,7 +167,7 @@ def tile_list_tabres_none_kernel(
         for s in range(SLICES):
             make_h(s)
 
-        results = [keep.tile([P, S], F32, name=f"result{b}", align_bytes=64) for b in range(BLOCKS)]
+        results = [keep.tile([P, S], F32, name=f"result{b}", align_bytes=LINE) for b in range(BLOCKS)]
 
         def gather(b, lo, hi):
             nc.vector.tensor_copy(results[b][:, lo:hi], residual[b][:].indirect(listed(lo, hi)))
@@ -206,17 +207,17 @@ def tile_list_tabres_none_kernel(
             store(b, 0, S)
 
         def staged(b, place):
-            return stream.tile([P, S], F32, name=f"product{b}", offset=place, align_bytes=64)
+            return stream.tile([P, S], F32, name=f"product{b}", offset=place, align_bytes=LINE)
 
         finish(0, staged(0, late_at), w4_planes, 0)
-        late_planes = stream.tile([P, PASSES, (M - EARLY * P) // 4], I32, name="late_planes", offset=late_at, align_bytes=64)
+        late_planes = stream.tile([P, PASSES, (M - EARLY * P) // 4], I32, name="late_planes", offset=late_at, align_bytes=LINE)
         nc.gpsimd.memset(late_planes[:], 0)
         load_planes(nc.sync, late_planes, EARLY * P, M)
         gather(1, 0, S)
         for s in range(SLICES):
             cols = slice(s * BANK, (s + 1) * BANK)
             place = (6 * SLOT - 2 * BANK, places[0], late_at + 4 * S)[s]
-            part = stream.tile([P, BANK], F32, name=f"part{s}", offset=place, align_bytes=64)
+            part = stream.tile([P, BANK], F32, name=f"part{s}", offset=place, align_bytes=LINE)
             nc.scalar.copy(out=part[:], in_=make_y(1, s, w4_planes, 0)[:])
             nc.gpsimd.tensor_tensor(results[1][:, cols], results[1][:, cols], part[:], ADD)
         for b in range(5, BLOCKS):

@@ -46,11 +46,10 @@ def tile_list_tabres_none_kernel(
         def listed(lo, hi):
             return offsets[:, lo // GROUP : hi // GROUP]
 
-        tab_planes = [keep.tile([P, T // 4], I32, name=f"tab_planes{a}", align_bytes=LINE) for a in range(PASSES)]
+        tab_planes = keep.tile([P, PASSES * T // 4], I32, name="tab_planes", align_bytes=LINE)
         w4_planes = keep.tile([P, PASSES, EARLY * P // 4], I32, name="w4_planes", align_bytes=LINE)
         nc.vector.memset(w4_planes[:], 0)
-        for planes in tab_planes:
-            nc.vector.memset(planes[:], 0)
+        nc.vector.memset(tab_planes[:], 0)
         moved = keep.tile([P, PASSES, S // 4], I32, name="moved", align_bytes=LINE)
         nc.vector.memset(moved[:], 0)
 
@@ -72,10 +71,13 @@ def tile_list_tabres_none_kernel(
         late_at = 7 * SLOT
         places = [slot * SLOT for slot in (0, 1, 2, 3, 4, 5, 6, 0)]
 
-        def load_residual(b):
-            rows = stream.tile([P, T], F32, name=f"residual{b}", offset=places[b], align_bytes=LINE)
-            nc.sync.dma_start(out=rows[:], in_=rT[b * P : (b + 1) * P, :])
-            residual.append(rows)
+        def load_residual(b, count=1):
+            rows = stream.tile([P, count * T], F32, name=f"residual{b}", offset=places[b], align_bytes=LINE)
+            nc.sync.dma_start(
+                out=rows[:].rearrange("p (c t) -> p c t", c=count),
+                in_=rT[b * P : (b + count) * P, :].rearrange("(c p) t -> p c t", p=P),
+            )
+            residual.extend(rows[:, c * T : (c + 1) * T] for c in range(count))
 
         down_raw = stream.tile([P, PASSES, PACK, R], F32, name="down_raw", offset=0, align_bytes=LINE)
 
@@ -86,20 +88,23 @@ def tile_list_tabres_none_kernel(
             )
 
         load_down(0)
-        for a in range(PASSES):
-            nc.sync.dma_start(out=tab_planes[a][32:96:4, :], in_=tab_scales[a].bitcast(I32))
+        nc.sync.dma_start(
+            out=tab_planes[32:96:4, :].rearrange("q (a c) -> q a c", a=PASSES),
+            in_=tab_scales.bitcast(I32).rearrange("a q c -> q a c"),
+        )
         tab0 = load_table(0)
         load_down(1)
         tab1 = load_table(1)
-        up_raw = stream.tile([P, PACK, M], F32, name="up_raw", offset=3 * SLOT, align_bytes=LINE)
+        up_raw = stream.tile([P, PACK, M], F32, name="up_raw", offset=4 * SLOT, align_bytes=LINE)
         nc.sync.dma_start(out=up_raw[:], in_=up.rearrange("(p i) n -> p i n", i=PACK))
-        for b in range(4):
-            load_residual(b)
+        load_residual(0)
+        load_residual(1)
+        load_residual(2, 2)
 
         v_words = [keep.tile([P, S], U32, name=f"v_words{a}", align_bytes=LINE) for a in range(PASSES)]
         both = keep.tile([P, PASSES, S], U8, name="both", align_bytes=LINE)
         for a in range(PASSES):
-            nc.vector.tensor_copy(both[:, a, :], tab_planes[a][:].bitcast(U8).indirect(offsets[:]))
+            nc.vector.tensor_copy(both[:, a, :], tab_planes[:].bitcast(U8)[:, a * T : (a + 1) * T].indirect(offsets[:]))
         for r in range(4):
             nc.scalar.dma_start(out=moved[r:P:32, :, :], in_=both[32 + 4 * r : 96 : 16, :, :].bitcast(I32))
         v_scales = [moved[:, a, :].bitcast(U8) for a in range(PASSES)]
@@ -153,7 +158,7 @@ def tile_list_tabres_none_kernel(
         def make_up(half):
             cols = slice(half * BANK, (half + 1) * BANK)
             grouped = stream.tile(
-                [P, PACK * BANK], BF16, name=f"up_bf{half}", offset=4 * SLOT + half * 2 * PACK * BANK, align_bytes=LINE
+                [P, PACK * BANK], BF16, name=f"up_bf{half}", offset=5 * SLOT + half * 2 * PACK * BANK, align_bytes=LINE
             )
             nc.vector.tensor_copy(
                 out=grouped[:].rearrange("p (c j i) -> p c i j", j=4, i=PACK),
@@ -167,13 +172,17 @@ def tile_list_tabres_none_kernel(
         for s in range(SLICES):
             make_h(s)
 
-        results = [keep.tile([P, S], F32, name=f"result{b}", align_bytes=LINE) for b in range(BLOCKS)]
+        all_results = keep.tile([P, BLOCKS * S], F32, name="all_results", align_bytes=LINE)
+        results = [all_results[:, b * S : (b + 1) * S] for b in range(BLOCKS)]
 
         def gather(b, lo, hi):
-            nc.vector.tensor_copy(results[b][:, lo:hi], residual[b][:].indirect(listed(lo, hi)))
+            nc.vector.tensor_copy(results[b][:, lo:hi], residual[b].indirect(listed(lo, hi)))
 
-        def store(b, lo, hi):
-            nc.sync.dma_start(out=out[b * P : (b + 1) * P, lo:hi], in_=results[b][:, lo:hi])
+        def store(b, count=1):
+            nc.sync.dma_start(
+                out=out[b * P : (b + count) * P, :].rearrange("(c p) s -> p c s", p=P),
+                in_=all_results[:, b * S : (b + count) * S].rearrange("p (c s) -> p c s", c=count),
+            )
 
         def make_y(b, s, planes, first):
             cols = slice(s * BANK, (s + 1) * BANK)
@@ -203,13 +212,13 @@ def tile_list_tabres_none_kernel(
             for s in range(SLICES):
                 nc.scalar.copy(out=product[:, s * BANK : (s + 1) * BANK], in_=make_y(b, s, planes, first)[:])
             gather(b, 0, S)
-            nc.gpsimd.tensor_tensor(results[b][:], results[b][:], product[:], ADD)
-            store(b, 0, S)
+            nc.gpsimd.tensor_tensor(results[b], results[b], product[:], ADD)
 
         def staged(b, place):
             return stream.tile([P, S], F32, name=f"product{b}", offset=place, align_bytes=LINE)
 
         finish(0, staged(0, late_at), w4_planes, 0)
+        store(0)
         late_planes = stream.tile([P, PASSES, (M - EARLY * P) // 4], I32, name="late_planes", offset=late_at, align_bytes=LINE)
         nc.gpsimd.memset(late_planes[:], 0)
         load_planes(nc.sync, late_planes, EARLY * P, M)
@@ -222,10 +231,9 @@ def tile_list_tabres_none_kernel(
             nc.gpsimd.tensor_tensor(results[1][:, cols], results[1][:, cols], part[:], ADD)
         for b in range(5, BLOCKS):
             load_residual(b)
-        store(1, 0, S)
         last = BLOCKS - 1
         for b in range(2, last):
-            product = staged(b, places[1 + (b - 2) % 4] + (b - 2) // 4 * 4 * S)
+            product = staged(b, places[b // 2] + b % 2 * 4 * S)
             if b < EARLY:
                 finish(b, product, w4_planes, 0)
             else:
@@ -237,4 +245,7 @@ def tile_list_tabres_none_kernel(
             if s > 0:
                 lo, hi = (s - 1) * BANK, s * BANK
                 nc.vector.tensor_tensor(results[last][:, lo:hi], banks[s - 1][:], results[last][:, lo:hi], ADD)
-        store(last, 0, S)
+        store(1, 3)
+        store(4, 2)
+        store(6)
+        store(last)

@@ -24,9 +24,12 @@ SLICES = S // BANK
 BLOCKS = M // P
 GROUP = 16
 SLOT = 4 * T
+ROW = 4 * S
 EARLY = 3
-STAGE_BUFS = 3
 LINE = 256
+WORDS = 7 * SLOT
+PLANES = WORDS + 2 * ROW
+ASIDE = PLANES + ROW // 2
 
 
 def tile_list_tabres_none_kernel(
@@ -36,7 +39,7 @@ def tile_list_tabres_none_kernel(
     with ExitStack() as ctx:
         keep = ctx.enter_context(tc.tile_pool(name="keep", bufs=1))
         stream = ctx.enter_context(tc.tile_pool(name="stream", bufs=1))
-        stage = ctx.enter_context(tc.tile_pool(name="stage", bufs=STAGE_BUFS))
+        stage = ctx.enter_context(tc.tile_pool(name="stage", bufs=3))
         psum_h = ctx.enter_context(tc.psum_pool(name="psum_h", bufs=3))
         psum_y = ctx.enter_context(tc.psum_pool(name="psum_y", bufs=5))
 
@@ -46,90 +49,115 @@ def tile_list_tabres_none_kernel(
         def listed(lo, hi):
             return offsets[:, lo // GROUP : hi // GROUP]
 
-        tab_planes = keep.tile([P, PASSES * T // 4], I32, name="tab_planes", align_bytes=LINE)
-        w4_planes = keep.tile([P, PASSES, EARLY * P // 4], I32, name="w4_planes", align_bytes=LINE)
-        nc.vector.memset(w4_planes[:], 0)
-        nc.vector.memset(tab_planes[:], 0)
-        moved = keep.tile([P, PASSES, S // 4], I32, name="moved", align_bytes=LINE)
-        nc.vector.memset(moved[:], 0)
-
-        def load_planes(engine, planes, lo, hi):
-            rows = w4_scales.bitcast(I32).rearrange("a (q r) c -> r q a c", r=4)
-            for r in range(4):
-                engine.dma_start(out=planes[r:P:32, :, :], in_=rows[r][:, :, lo // 4 : hi // 4])
-
         w4 = keep.tile([P, PASSES, 2 * M // 4], I32, name="w4", align_bytes=LINE)
         nc.sync.dma_start(out=w4[:], in_=w4_words.bitcast(I32).rearrange("a p c -> p a c"))
-        load_planes(nc.sync, w4_planes, 0, EARLY * P)
+
+        early_planes = keep.tile([P, PASSES, EARLY * P // 4], I32, name="early_planes", align_bytes=LINE)
+        raw_scales = stream.tile([P, PASSES * T // 4], I32, name="raw_scales", offset=2 * SLOT, align_bytes=LINE)
+        nc.vector.memset(early_planes[:], 0)
+        nc.vector.memset(raw_scales[:], 0)
+
+        def load_planes(planes, lo, hi):
+            rows = w4_scales.bitcast(I32).rearrange("a (q r) c -> r q a c", r=4)
+            for r in range(4):
+                nc.sync.dma_start(out=planes[r:P:32, :, :], in_=rows[r][:, :, lo // 4 : hi // 4])
+
+        load_planes(early_planes, 0, EARLY * P)
+
+        def place(shape, dtype, name, at):
+            return stream.tile(shape, dtype, name=name, offset=at, align_bytes=LINE)
 
         def load_table(a):
-            words = stream.tile([P, T], I32, name=f"tab{a}", offset=(1 + a) * SLOT, align_bytes=LINE)
+            words = place([P, T], I32, f"tab{a}", a * SLOT)
             nc.sync.dma_start(out=words[:], in_=tab_words[a].rearrange("p t i -> p (t i)").bitcast(I32))
             return words
 
+        def load_down(a):
+            rows = place([P, PACK, R], F32, f"down_raw{a}", (PLANES, 2 * SLOT + SLOT // 2)[a])
+            nc.sync.dma_start(
+                out=rows[:], in_=down[a * K_PASS : (a + 1) * K_PASS, :].rearrange("(p i) r -> p i r", i=PACK)
+            )
+            return rows
+
         residual = []
-        late_at = 7 * SLOT
-        places = [slot * SLOT for slot in (0, 1, 2, 3, 4, 5, 6, 0)]
+        slots = (0, 1, 6, 2, 3, 4, 0, 5)
 
         def load_residual(b, count=1):
-            rows = stream.tile([P, count * T], F32, name=f"residual{b}", offset=places[b], align_bytes=LINE)
+            rows = place([P, count * T], F32, f"residual{b}", slots[b] * SLOT)
             nc.sync.dma_start(
                 out=rows[:].rearrange("p (c t) -> p c t", c=count),
                 in_=rT[b * P : (b + count) * P, :].rearrange("(c p) t -> p c t", p=P),
             )
             residual.extend(rows[:, c * T : (c + 1) * T] for c in range(count))
 
-        down_raw = stream.tile([P, PASSES, PACK, R], F32, name="down_raw", offset=0, align_bytes=LINE)
-
-        def load_down(a):
-            nc.sync.dma_start(
-                out=down_raw[:, a, :, :],
-                in_=down[a * K_PASS : (a + 1) * K_PASS, :].rearrange("(p i) r -> p i r", i=PACK),
-            )
-
-        load_down(0)
         nc.sync.dma_start(
-            out=tab_planes[32:96:4, :].rearrange("q (a c) -> q a c", a=PASSES),
+            out=raw_scales[32:96:4, :].rearrange("q (a c) -> q a c", a=PASSES),
             in_=tab_scales.bitcast(I32).rearrange("a q c -> q a c"),
         )
+        down_raw = [load_down(a) for a in range(PASSES)]
         tab0 = load_table(0)
-        load_down(1)
         tab1 = load_table(1)
-        up_raw = stream.tile([P, PACK, M], F32, name="up_raw", offset=4 * SLOT, align_bytes=LINE)
-        nc.sync.dma_start(out=up_raw[:], in_=up.rearrange("(p i) n -> p i n", i=PACK))
-        load_residual(0)
-        load_residual(1)
-        load_residual(2, 2)
 
-        v_words = [keep.tile([P, S], U32, name=f"v_words{a}", align_bytes=LINE) for a in range(PASSES)]
-        both = keep.tile([P, PASSES, S], U8, name="both", align_bytes=LINE)
+        picked_scales = keep.tile([P, PASSES, S], U8, name="picked_scales", align_bytes=LINE)
         for a in range(PASSES):
-            nc.vector.tensor_copy(both[:, a, :], tab_planes[:].bitcast(U8)[:, a * T : (a + 1) * T].indirect(offsets[:]))
-        for r in range(4):
-            nc.scalar.dma_start(out=moved[r:P:32, :, :], in_=both[32 + 4 * r : 96 : 16, :, :].bitcast(I32))
-        v_scales = [moved[:, a, :].bitcast(U8) for a in range(PASSES)]
-        nc.vector.tensor_copy(v_words[0][:], tab0[:].bitcast(U32).indirect(offsets[:]))
-
+            nc.vector.tensor_copy(
+                picked_scales[:, a, :], raw_scales[:].bitcast(U8)[:, a * T : (a + 1) * T].indirect(offsets[:])
+            )
         down_codes = keep.tile([P, PASSES, R], U32, name="down_codes", align_bytes=LINE)
         down_scales = keep.tile([P, PASSES, R], U8, name="down_scales", align_bytes=LINE)
-        for a in range(PASSES):
-            grouped = stage.tile([P, PACK * R], BF16, name=f"down_bf{a}", tag="stage", align_bytes=LINE)
+
+        def round_down(a, at):
+            grouped = place([P, PACK * R], BF16, f"down_bf{a}", at)
             nc.scalar.copy(
                 out=grouped[:].rearrange("p (t m i) -> p m t i", t=PACK, i=PACK),
-                in_=down_raw[:, a, :, :].rearrange("p i (m t) -> p m t i", t=PACK),
+                in_=down_raw[a][:].rearrange("p i (m t) -> p m t i", t=PACK),
             )
+            return grouped
+
+        def quantise_down(a, grouped):
             nc.vector.quantize_mx(
                 out=down_codes[:, a, :].bitcast(FP8X4), scales=down_scales[:, a, :], in_=grouped[:]
             )
 
+        rounded = [round_down(0, ASIDE + 2 * ROW), round_down(1, WORDS - 2048)]
+        v_planes = place([P, PASSES, S // 4], I32, "v_planes", PLANES)
+        nc.vector.memset(v_planes[:], 0)
+        for r in range(4):
+            nc.scalar.dma_start(
+                out=v_planes[r:P:32, :, :], in_=picked_scales[32 + 4 * r : 96 : 16, :, :].bitcast(I32)
+            )
+        v_scales = [v_planes[:, a, :].bitcast(U8) for a in range(PASSES)]
+        for a in range(PASSES):
+            quantise_down(a, rounded[a])
+        up_raw = place([P, PACK, M], F32, "up_raw", 6 * SLOT)
+        nc.sync.dma_start(out=up_raw[:], in_=up.rearrange("(p i) n -> p i n", i=PACK))
+        picked_words = place([P, PASSES, S], U32, "picked_words", WORDS)
+        v_words = [picked_words[:, a, :] for a in range(PASSES)]
+        nc.vector.tensor_copy(v_words[0], tab0[:].bitcast(U32).indirect(offsets[:]))
+        load_residual(0)
+
         for s in range(SLICES):
             lo, hi = s * BANK, (s + 1) * BANK
             nc.vector.tensor_copy(v_words[1][:, lo:hi], tab1[:].bitcast(U32).indirect(listed(lo, hi)))
+        load_residual(1)
+
+        up_codes = keep.tile([P, M], U32, name="up_codes", align_bytes=LINE)
+        up_scales = keep.tile([P, M], U8, name="up_scales", align_bytes=LINE)
+        for half in range(M // BANK):
+            cols = slice(half * BANK, (half + 1) * BANK)
+            grouped = place([P, PACK * BANK], BF16, f"up_bf{half}", (ASIDE + ROW, 2 * SLOT)[half])
+            nc.vector.tensor_copy(
+                out=grouped[:].rearrange("p (c j i) -> p c i j", j=4, i=PACK),
+                in_=up_raw[:, :, cols].rearrange("p i (c j) -> p c i j", j=4),
+            )
+            nc.vector.quantize_mx(out=up_codes[:, cols].bitcast(FP8X4), scales=up_scales[:, cols], in_=grouped[:])
+
+        load_residual(2)
+        load_residual(3)
 
         h_codes = keep.tile([P, S], U32, name="h_codes", align_bytes=LINE)
         h_scales = keep.tile([P, S], U8, name="h_scales", align_bytes=LINE)
-
-        def make_h(s):
+        for s in range(SLICES):
             grouped = stage.tile([P, BANK, PACK], BF16, name=f"h_bf{s}", tag="stage", align_bytes=LINE)
             for c in range(BANK // P):
                 cols = slice(s * BANK + c * P, s * BANK + (c + 1) * P)
@@ -152,31 +180,8 @@ def tile_list_tabres_none_kernel(
                 in_=grouped[:].rearrange("p n t -> p (n t)"),
             )
 
-        up_codes = keep.tile([P, M], U32, name="up_codes", align_bytes=LINE)
-        up_scales = keep.tile([P, M], U8, name="up_scales", align_bytes=LINE)
-
-        def make_up(half):
-            cols = slice(half * BANK, (half + 1) * BANK)
-            grouped = stream.tile(
-                [P, PACK * BANK], BF16, name=f"up_bf{half}", offset=5 * SLOT + half * 2 * PACK * BANK, align_bytes=LINE
-            )
-            nc.vector.tensor_copy(
-                out=grouped[:].rearrange("p (c j i) -> p c i j", j=4, i=PACK),
-                in_=up_raw[:, :, cols].rearrange("p i (c j) -> p c i j", j=4),
-            )
-            nc.vector.quantize_mx(out=up_codes[:, cols].bitcast(FP8X4), scales=up_scales[:, cols], in_=grouped[:])
-
-        make_up(0)
-        make_up(1)
-        load_residual(4)
-        for s in range(SLICES):
-            make_h(s)
-
         all_results = keep.tile([P, BLOCKS * S], F32, name="all_results", align_bytes=LINE)
         results = [all_results[:, b * S : (b + 1) * S] for b in range(BLOCKS)]
-
-        def gather(b, lo, hi):
-            nc.vector.tensor_copy(results[b][:, lo:hi], residual[b].indirect(listed(lo, hi)))
 
         def store(b, count=1):
             nc.sync.dma_start(
@@ -208,44 +213,39 @@ def tile_list_tabres_none_kernel(
                 )
             return acc
 
-        def finish(b, product, planes, first):
+        def product(b, planes, first):
             for s in range(SLICES):
-                nc.scalar.copy(out=product[:, s * BANK : (s + 1) * BANK], in_=make_y(b, s, planes, first)[:])
-            gather(b, 0, S)
-            nc.gpsimd.tensor_tensor(results[b], results[b], product[:], ADD)
+                nc.scalar.copy(out=results[b][:, s * BANK : (s + 1) * BANK], in_=make_y(b, s, planes, first)[:])
 
-        def staged(b, place):
-            return stream.tile([P, S], F32, name=f"product{b}", offset=place, align_bytes=LINE)
+        def add_residual(b, at, lo=0, hi=S):
+            picked = place([P, hi - lo], F32, f"picked{b}_{lo}", at)
+            nc.vector.tensor_copy(picked[:], residual[b].indirect(listed(lo, hi)))
+            nc.gpsimd.tensor_tensor(results[b][:, lo:hi], results[b][:, lo:hi], picked[:], ADD)
 
-        finish(0, staged(0, late_at), w4_planes, 0)
+        for b in range(EARLY):
+            product(b, early_planes, 0)
+        add_residual(0, ASIDE)
         store(0)
-        late_planes = stream.tile([P, PASSES, (M - EARLY * P) // 4], I32, name="late_planes", offset=late_at, align_bytes=LINE)
+        late_planes = place([P, PASSES, (M - EARLY * P) // 4], I32, "late_planes", ASIDE)
         nc.gpsimd.memset(late_planes[:], 0)
-        load_planes(nc.sync, late_planes, EARLY * P, M)
-        gather(1, 0, S)
+        load_planes(late_planes, EARLY * P, M)
         for s in range(SLICES):
-            cols = slice(s * BANK, (s + 1) * BANK)
-            place = (6 * SLOT - 2 * BANK, places[0], late_at + 4 * S)[s]
-            part = stream.tile([P, BANK], F32, name=f"part{s}", offset=place, align_bytes=LINE)
-            nc.scalar.copy(out=part[:], in_=make_y(1, s, w4_planes, 0)[:])
-            nc.gpsimd.tensor_tensor(results[1][:, cols], results[1][:, cols], part[:], ADD)
-        for b in range(5, BLOCKS):
-            load_residual(b)
+            add_residual(1, slots[4 + s] * SLOT, s * BANK, (s + 1) * BANK)
+            load_residual(4 + s)
+        add_residual(2, slots[7] * SLOT)
+        load_residual(7)
         last = BLOCKS - 1
-        for b in range(2, last):
-            product = staged(b, places[b // 2] + b % 2 * 4 * S)
-            if b < EARLY:
-                finish(b, product, w4_planes, 0)
-            else:
-                finish(b, product, late_planes, EARLY)
+        for b in range(EARLY, last):
+            product(b, late_planes, EARLY)
+            add_residual(b, ASIDE + ROW + b % 2 * ROW)
         banks = [make_y(last, s, late_planes, EARLY) for s in range(SLICES)]
         for s in range(SLICES + 1):
             if s < SLICES:
-                gather(last, s * BANK, (s + 1) * BANK)
+                lo, hi = s * BANK, (s + 1) * BANK
+                nc.vector.tensor_copy(results[last][:, lo:hi], residual[last].indirect(listed(lo, hi)))
             if s > 0:
                 lo, hi = (s - 1) * BANK, s * BANK
                 nc.vector.tensor_tensor(results[last][:, lo:hi], banks[s - 1][:], results[last][:, lo:hi], ADD)
-        store(1, 3)
-        store(4, 2)
-        store(6)
+        store(1, 4)
+        store(5, 2)
         store(last)

@@ -183,8 +183,8 @@ def tile_list_tabres_none_kernel(
         all_results = keep.tile([P, BLOCKS * S], F32, name="all_results", align_bytes=LINE)
         results = [all_results[:, b * S : (b + 1) * S] for b in range(BLOCKS)]
 
-        def store(b, count=1):
-            nc.sync.dma_start(
+        def store(b, count=1, queue=nc.sync):
+            queue.dma_start(
                 out=out[b * P : (b + count) * P, :].rearrange("(c p) s -> p c s", p=P),
                 in_=all_results[:, b * S : (b + count) * S].rearrange("p (c s) -> p c s", c=count),
             )
@@ -247,5 +247,5 @@ def tile_list_tabres_none_kernel(
                 lo, hi = (s - 1) * BANK, s * BANK
                 nc.vector.tensor_tensor(results[last][:, lo:hi], banks[s - 1][:], results[last][:, lo:hi], ADD)
         store(1, 4)
-        store(5, 2)
+        store(5, 2, nc.scalar)
         store(last)

@@ -44,13 +44,12 @@ def tile_list_tabres_none_kernel(
         psum_y = ctx.enter_context(tc.psum_pool(name="psum_y", bufs=5))
 
         offsets = keep.tile([P, S // GROUP], U16, name="offsets")
+        w4 = keep.tile([P, PASSES, 2 * M // 4], I32, name="w4", align_bytes=LINE)
+        nc.sync.dma_start(out=w4[:], in_=w4_words.bitcast(I32).rearrange("a p c -> p a c"))
         nc.sync.dma_start(offsets[:], offs)
 
         def listed(lo, hi):
             return offsets[:, lo // GROUP : hi // GROUP]
-
-        w4 = keep.tile([P, PASSES, 2 * M // 4], I32, name="w4", align_bytes=LINE)
-        nc.sync.dma_start(out=w4[:], in_=w4_words.bitcast(I32).rearrange("a p c -> p a c"))
 
         early_planes = keep.tile([P, PASSES, EARLY * P // 4], I32, name="early_planes", align_bytes=LINE)
         raw_scales = stream.tile([P, PASSES * T // 4], I32, name="raw_scales", offset=2 * SLOT, align_bytes=LINE)

from contextlib import ExitStack

import concourse.mybir as mybir

K, M, T, S, R = 1024, 1024, 4096, 1536, 512
FLOPS = 2 * S * (K * R + K * M + R * M)

F32 = mybir.dt.float32
BF16 = mybir.dt.bfloat16
I32 = mybir.dt.int32
U32 = mybir.dt.uint32
U16 = mybir.dt.uint16
U8 = mybir.dt.uint8
FP8X4 = mybir.dt.float8_e4m3fn_x4
FP4X4 = mybir.dt.float4_e2m1fn_x4
ADD = mybir.AluOpType.add

P = 128
PACK = 4
K_PASS = P * PACK
PASSES = K // K_PASS
BANK = 512
SLICES = S // BANK
BLOCKS = M // P
GROUP = 16
SLOT = 4 * T
ROW = 4 * S
EARLY = 3
LINE = 256
WORDS = 7 * SLOT
PLANES = WORDS + 2 * ROW
ASIDE = PLANES + ROW // 2


def tile_list_tabres_none_kernel(
    tc, tab_words, tab_scales, w4_words, w4_scales, down, up, rT, offs, out
):
    nc = tc.nc
    with ExitStack() as ctx:
        keep = ctx.enter_context(tc.tile_pool(name="keep", bufs=1))
        stream = ctx.enter_context(tc.tile_pool(name="stream", bufs=1))
        stage = ctx.enter_context(tc.tile_pool(name="stage", bufs=3))
        psum_h = ctx.enter_context(tc.psum_pool(name="psum_h", bufs=3))
        psum_y = ctx.enter_context(tc.psum_pool(name="psum_y", bufs=5))

        offsets = keep.tile([P, S // GROUP], U16, name="offsets")
        w4 = keep.tile([P, PASSES, 2 * M // 4], I32, name="w4", align_bytes=LINE)
        nc.sync.dma_start(out=w4[:], in_=w4_words.bitcast(I32).rearrange("a p c -> p a c"))
        nc.sync.dma_start(offsets[:], offs)

        def listed(lo, hi):
            return offsets[:, lo // GROUP : hi // GROUP]

        early_planes = keep.tile([P, PASSES, EARLY * P // 4], I32, name="early_planes", align_bytes=LINE)
        raw_scales = stream.tile([P, PASSES * T // 4], I32, name="raw_scales", offset=2 * SLOT, align_bytes=LINE)
        nc.vector.memset(early_planes[:], 0)
        nc.vector.memset(raw_scales[:], 0)

        def load_planes(planes, lo, hi):
            rows = w4_scales.bitcast(I32).rearrange("a (q r) c -> r q a c", r=4)
            for r in range(4):
                nc.sync.dma_start(out=planes[r:P:32, :, :], in_=rows[r][:, :, lo // 4 : hi // 4])

        load_planes(early_planes, 0, EARLY * P)

        def place(shape, dtype, name, at):
            return stream.tile(shape, dtype, name=name, offset=at, align_bytes=LINE)

        def load_table(a):
            words = place([P, T], I32, f"tab{a}", a * SLOT)
            nc.sync.dma_start(out=words[:], in_=tab_words[a].rearrange("p t i -> p (t i)").bitcast(I32))
            return words

        def load_down(a):
            rows = place([P, PACK, R], F32, f"down_raw{a}", (PLANES, 2 * SLOT + SLOT // 2)[a])
            nc.sync.dma_start(
                out=rows[:], in_=down[a * K_PASS : (a + 1) * K_PASS, :].rearrange("(p i) r -> p i r", i=PACK)
            )
            return rows

        residual = []
        slots = (0, 1, 6, 2, 3, 4, 0, 5)

        def load_residual(b, count=1):
            rows = place([P, count * T], F32, f"residual{b}", slots[b] * SLOT)
            nc.sync.dma_start(
                out=rows[:].rearrange("p (c t) -> p c t", c=count),
                in_=rT[b * P : (b + count) * P, :].rearrange("(c p) t -> p c t", p=P),
            )
            residual.extend(rows[:, c * T : (c + 1) * T] for c in range(count))

        nc.sync.dma_start(
            out=raw_scales[32:96:4, :].rearrange("q (a c) -> q a c", a=PASSES),
            in_=tab_scales.bitcast(I32).rearrange("a q c -> q a c"),
        )
        down_raw = [load_down(a) for a in range(PASSES)]
        tab0 = load_table(0)
        tab1 = load_table(1)

        picked_scales = keep.tile([P, PASSES, S], U8, name="picked_scales", align_bytes=LINE)
        for a in range(PASSES):
            nc.vector.tensor_copy(
                picked_scales[:, a, :], raw_scales[:].bitcast(U8)[:, a * T : (a + 1) * T].indirect(offsets[:])
            )
        down_codes = keep.tile([P, PASSES, R], U32, name="down_codes", align_bytes=LINE)
        down_scales = keep.tile([P, PASSES, R], U8, name="down_scales", align_bytes=LINE)

        def round_down(a, at):
            grouped = place([P, PACK * R], BF16, f"down_bf{a}", at)
            nc.scalar.copy(
                out=grouped[:].rearrange("p (t m i) -> p m t i", t=PACK, i=PACK),
                in_=down_raw[a][:].rearrange("p i (m t) -> p m t i", t=PACK),
            )
            return grouped

        def quantise_down(a, grouped):
            nc.vector.quantize_mx(
                out=down_codes[:, a, :].bitcast(FP8X4), scales=down_scales[:, a, :], in_=grouped[:]
            )

        rounded = [round_down(0, ASIDE + 2 * ROW), round_down(1, WORDS - 2048)]
        v_planes = place([P, PASSES, S // 4], I32, "v_planes", PLANES)
        nc.vector.memset(v_planes[:], 0)
        for r in range(4):
            nc.scalar.dma_start(
                out=v_planes[r:P:32, :, :], in_=picked_scales[32 + 4 * r : 96 : 16, :, :].bitcast(I32)
            )
        v_scales = [v_planes[:, a, :].bitcast(U8) for a in range(PASSES)]
        for a in range(PASSES):
            quantise_down(a, rounded[a])
        up_raw = place([P, PACK, M], F32, "up_raw", 6 * SLOT)
        nc.sync.dma_start(out=up_raw[:], in_=up.rearrange("(p i) n -> p i n", i=PACK))
        picked_words = place([P, PASSES, S], U32, "picked_words", WORDS)
        v_words = [picked_words[:, a, :] for a in range(PASSES)]
        nc.vector.tensor_copy(v_words[0], tab0[:].bitcast(U32).indirect(offsets[:]))
        load_residual(0)

        for s in range(SLICES):
            lo, hi = s * BANK, (s + 1) * BANK
            nc.vector.tensor_copy(v_words[1][:, lo:hi], tab1[:].bitcast(U32).indirect(listed(lo, hi)))
        load_residual(1)

        up_codes = keep.tile([P, M], U32, name="up_codes", align_bytes=LINE)
        up_scales = keep.tile([P, M], U8, name="up_scales", align_bytes=LINE)
        for half in range(M // BANK):
            cols = slice(half * BANK, (half + 1) * BANK)
            grouped = place([P, PACK * BANK], BF16, f"up_bf{half}", (ASIDE + ROW, 2 * SLOT)[half])
            nc.vector.tensor_copy(
                out=grouped[:].rearrange("p (c j i) -> p c i j", j=4, i=PACK),
                in_=up_raw[:, :, cols].rearrange("p i (c j) -> p c i j", j=4),
            )
            nc.vector.quantize_mx(out=up_codes[:, cols].bitcast(FP8X4), scales=up_scales[:, cols], in_=grouped[:])

        load_residual(2)
        load_residual(3)

        h_codes = keep.tile([P, S], U32, name="h_codes", align_bytes=LINE)
        h_scales = keep.tile([P, S], U8, name="h_scales", align_bytes=LINE)
        for s in range(SLICES):
            grouped = stage.tile([P, BANK, PACK], BF16, name=f"h_bf{s}", tag="stage", align_bytes=LINE)
            for c in range(BANK // P):
                cols = slice(s * BANK + c * P, s * BANK + (c + 1) * P)
                acc = psum_h.tile([P, PACK, P], F32, name="acc_h")
                for t in range(PACK):
                    for a in range(PASSES):
                        nc.tensor.matmul_mx(
                            out=acc[:, t, :],
                            lhsT=down_codes[:, a, t * P : (t + 1) * P].bitcast(FP8X4),
                            lhsT_scale=down_scales[:, a, t * P : (t + 1) * P],
                            rhs=v_words[a][:, cols].bitcast(FP8X4),
                            rhs_scale=v_scales[a][:, cols],
                            start=(a == 0),
                            stop=(a == PASSES - 1),
                        )
                nc.scalar.copy(out=grouped[:, c * P : (c + 1) * P, :], in_=acc[:].rearrange("p t n -> p n t"))
            nc.vector.quantize_mx(
                out=h_codes[:, s * BANK : (s + 1) * BANK].bitcast(FP8X4),
                scales=h_scales[:, s * BANK : (s + 1) * BANK],
                in_=grouped[:].rearrange("p n t -> p (n t)"),
            )

        all_results = keep.tile([P, BLOCKS * S], F32, name="all_results", align_bytes=LINE)
        results = [all_results[:, b * S : (b + 1) * S] for b in range(BLOCKS)]

        def store(b, count=1, queue=nc.sync):
            queue.dma_start(
                out=out[b * P : (b + count) * P, :].rearrange("(c p) s -> p c s", p=P),
                in_=all_results[:, b * S : (b + count) * S].rearrange("p (c s) -> p c s", c=count),
            )

        def make_y(b, s, planes, first):
            cols = slice(s * BANK, (s + 1) * BANK)
            acc = psum_y.tile([P, BANK], F32, name="acc_y")
            nc.tensor.matmul_mx(
                out=acc[:],
                lhsT=up_codes[:, P * b : P * (b + 1)].bitcast(FP8X4),
                lhsT_scale=up_scales[:, P * b : P * (b + 1)],
                rhs=h_codes[:, cols].bitcast(FP8X4),
                rhs_scale=h_scales[:, cols],
                start=True,
                stop=False,
            )
            for a in range(PASSES):
                nc.tensor.matmul_mx(
                    out=acc[:],
                    lhsT=w4[:, a, :].bitcast(U8)[:, 2 * P * b : 2 * P * (b + 1)].bitcast(FP4X4),
                    lhsT_scale=planes[:, a, :].bitcast(U8)[:, P * (b - first) : P * (b - first + 1)],
                    rhs=v_words[a][:, cols].bitcast(FP8X4),
                    rhs_scale=v_scales[a][:, cols],
                    start=False,
                    stop=(a == PASSES - 1),
                )
            return acc

        def product(b, planes, first):
            for s in range(SLICES):
                nc.scalar.copy(out=results[b][:, s * BANK : (s + 1) * BANK], in_=make_y(b, s, planes, first)[:])

        def add_residual(b, at, lo=0, hi=S):
            picked = place([P, hi - lo], F32, f"picked{b}_{lo}", at)
            nc.vector.tensor_copy(picked[:], residual[b].indirect(listed(lo, hi)))
            nc.gpsimd.tensor_tensor(results[b][:, lo:hi], results[b][:, lo:hi], picked[:], ADD)

        for b in range(EARLY):
            product(b, early_planes, 0)
        add_residual(0, ASIDE)
        store(0)
        late_planes = place([P, PASSES, (M - EARLY * P) // 4], I32, "late_planes", ASIDE)
        nc.gpsimd.memset(late_planes[:], 0)
        load_planes(late_planes, EARLY * P, M)
        for s in range(SLICES):
            add_residual(1, slots[4 + s] * SLOT, s * BANK, (s + 1) * BANK)
            load_residual(4 + s)
        add_residual(2, slots[7] * SLOT)
        load_residual(7)
        last = BLOCKS - 1
        for b in range(EARLY, last):
            product(b, late_planes, EARLY)
            add_residual(b, ASIDE + ROW + b % 2 * ROW)
        banks = [make_y(last, s, late_planes, EARLY) for s in range(SLICES)]
        for s in range(SLICES + 1):
            if s < SLICES:
                lo, hi = s * BANK, (s + 1) * BANK
                nc.vector.tensor_copy(results[last][:, lo:hi], residual[last].indirect(listed(lo, hi)))
            if s > 0:
                lo, hi = (s - 1) * BANK, s * BANK
                nc.vector.tensor_tensor(results[last][:, lo:hi], banks[s - 1][:], results[last][:, lo:hi], ADD)
        store(1, 4)
        store(5, 2, nc.scalar)
        store(last)
